import numpy as np
import ml_dtypes


def mxq(x, axis, fmt="e4m3"):
    dtype, down = {"e4m3": (ml_dtypes.float8_e4m3fn, 7), "e5m2": (ml_dtypes.float8_e5m2, 14)}[fmt]
    v = np.moveaxis(np.asarray(x, np.float32).astype(ml_dtypes.bfloat16).astype(np.float64), axis, -1)
    blocks = v.reshape(v.shape[:-1] + (-1, 32))
    amax = np.abs(blocks).max(-1, keepdims=True)
    byte = np.maximum(np.where(amax > 0, np.frexp(amax)[1] - 1 + 127, 0) - down, 1)
    scale = np.exp2(byte - 127.0)
    codes = (blocks / scale).astype(np.float32).astype(dtype).astype(np.float64)
    return np.moveaxis((codes * scale).reshape(v.shape), -1, axis)


WIDE = False


def mx_kscale(k):
    if not WIDE:
        return np.ones(k)
    levels = np.array([18, -18])
    if k % 512:
        return np.exp2(np.random.permutation(np.resize(levels, k // 32))).repeat(32)
    a = np.empty((k // 512, 16))
    for p in range(k // 512):
        a[p, :8] = np.random.permutation(np.resize(levels, 8))
        for g in range(8):
            far = levels[np.abs(levels - a[p, g]) >= 10]
            a[p, g + 8] = far[np.random.randint(len(far))]
    return np.exp2(a.ravel()).repeat(32)


def f64(x):
    return np.asarray(x).astype(np.float64)


def striped(idx):
    return np.tile(np.asarray(idx).reshape(-1, 16).T, (8, 1)).astype(np.uint16)


def unstriped(offs):
    return offs[:16].T.reshape(-1).astype(np.int64)

def planes(y):
    n, m = y.shape
    v = y.astype(np.float32).astype(ml_dtypes.bfloat16).astype(np.float64).reshape(n // 32, 32, m)
    top = np.abs(v).max(1)
    byte = np.clip(np.where(top > 0, np.frexp(top)[1] - 1 + 127 - 7, 1), 1, 254)
    codes = (v * np.exp2(127.0 - byte)[:, None, :]).reshape(n, m).astype(np.float32).astype(ml_dtypes.float8_e4m3fn).view(np.uint8)
    words = codes.reshape(n // 512, 128, 4, m).transpose(0, 1, 3, 2)
    return np.ascontiguousarray(words), np.ascontiguousarray(byte.astype(np.uint8).reshape(n // 512, 16, m))


N, T, D, V = 512, 2048, 512, 512


def setup_inputs():
    n = np.random.standard_normal
    idx = np.random.permutation(T)[:N]
    s = mx_kscale(D)[:, None]
    z = mx_kscale(V)[:, None]
    w = n((D, V)) / np.sqrt(D)
    return {
        "xT": (n((D, T)) / s).astype(np.float32),
        "wd": (w * s).astype(np.float32),
        "wv": (w.T / z).astype(np.float32),
        "y": (2 * np.random.randint(0, 2, (V, N)) - 1).astype(np.float32),
        "cw": (np.random.uniform(0.5, 1.5, (V, 1)) / np.sqrt(V) * z).astype(np.float32),
        "rw": np.tile(np.random.uniform(0.5, 1.5, N), (128, 1)).astype(np.float32),
        "offs": striped(idx),
    }


def reference(xT, wd, wv, y, cw, rw, offs):
    idx = unstriped(offs)
    a = mxq(f64(wd), 0, "e4m3").T @ mxq(f64(xT)[:, idx], 0, "e4m3")
    g = -f64(cw) * f64(rw)[:1] * f64(y) * np.maximum(1.0 - f64(y) * a, 0.0)
    dx = mxq(f64(wv), 0, "e4m3").T @ mxq(g, 0, "e5m2")
    gx = np.zeros((D, T))
    gx[:, idx] = dx
    out_0 = gx
    return (out_0,) + planes(out_0)

@@ -1,0 +1,216 @@
+from contextlib import ExitStack
+
+import concourse.mybir as mybir
+
+N, T, D, V = 512, 2048, 512, 512
+FLOPS = 2 * 2 * D * V * N
+
+F32 = mybir.dt.float32
+BF16 = mybir.dt.bfloat16
+I32 = mybir.dt.int32
+U32 = mybir.dt.uint32
+U16 = mybir.dt.uint16
+U8 = mybir.dt.uint8
+E4M3 = mybir.dt.float8_e4m3fn_x4
+E5M2 = mybir.dt.float8_e5m2_x4
+ALU = mybir.AluOpType
+ACT = mybir.ActivationFunctionType
+
+P = 128
+LANES = 4
+G_CHUNK = 128
+OUT_CHUNKS = (512, 512, 512, 256, 256)
+EARLY = N // 2
+
+
+def tile_attend_gml_pl_sqh_kernel(tc, xT, wd, wv, y, cw, rw, offs, out_0, out_1, out_2):
+    nc = tc.nc
+    with ExitStack() as ctx:
+        sb = ctx.enter_context(tc.tile_pool(name="sb", bufs=1))
+        ps = ctx.enter_context(tc.psum_pool(name="ps", bufs=1))
+
+        def tile(name, shape, dtype):
+            return sb.tile(shape, dtype, name=name, align_bytes=64)
+
+        x_rows = xT.rearrange("(p j) t -> p j t", j=LANES)
+        wd_rows = wd.rearrange("(p j) v -> p j v", j=LANES)
+        wv_rows = wv.rearrange("(p j) d -> p j d", j=LANES)
+        y_rows = y.rearrange("(p j) i -> p j i", j=LANES)
+        out_rows = out_0.rearrange("(p j) t -> p j t", j=LANES)
+        half = V // 2
+
+        offsets = sb.tile([P, N // 16], U16, name="offsets")
+        nc.sync.dma_start(offsets[:], offs)
+        cw_sb = tile("cw_sb", [P, LANES], F32)
+        nc.scalar.dma_start(cw_sb[:], cw.rearrange("(p j) o -> p (j o)", j=LANES))
+        x_plane = [tile("x_plane%d" % j, [P, T], F32) for j in range(LANES)]
+        for j in range(LANES):
+            nc.sync.dma_start(x_plane[j][:], x_rows[:, j, :])
+        wd_raw = [tile("wd_raw%d" % h, [P, LANES, half], F32) for h in range(2)]
+        for h in range(2):
+            nc.sync.dma_start(wd_raw[h][:], wd_rows[:, :, h * half : (h + 1) * half])
+        rw_sb = tile("rw_sb", [P, N], F32)
+        nc.sync.dma_start(rw_sb[:], rw)
+        y_sb = [tile("y_sb%d" % r, [P, N], F32) for r in range(LANES)]
+        for r in range(LANES):
+            nc.sync.dma_start(y_sb[r][:], y_rows[:, r, :])
+        wv_raw = [tile("wv_raw%d" % h, [P, LANES, half], F32) for h in range(2)]
+        for h in range(2):
+            nc.sync.dma_start(wv_raw[h][:], wv_rows[:, :, h * half : (h + 1) * half])
+
+        window = [tile("window%d" % t, [P, T], F32) for t in range(LANES)]
+        for t in range(LANES):
+            nc.vector.memset(window[t][:], 0.0)
+        neg_cw = tile("neg_cw", [P, LANES], F32)
+        nc.scalar.mul(neg_cw[:], cw_sb[:], -1.0)
+
+        x_b = tile("x_b", [P, N, LANES], BF16)
+        for j in range(LANES):
+            nc.vector.tensor_copy(x_b[:, :, j], x_plane[j][:].indirect(offsets[:]))
+        x_q = tile("x_q", [P, N], U32)
+        x_s = tile("x_s", [P, N], U8)
+        nc.vector.quantize_mx(out=x_q[:].bitcast(E4M3), scales=x_s[:], in_=x_b[:].rearrange("p n j -> p (n j)"))
+
+        def deal(copy, dealt, raw, h):
+            s_half = slice(h * P // 2, (h + 1) * P // 2)
+            copy(dealt[:, :, s_half, :].rearrange("p r s j -> p s j r"), raw[:].rearrange("p j (s r) -> p s j r", r=LANES))
+
+        def quantize_head(dealt, codes, scales, r):
+            nc.vector.quantize_mx(
+                out=codes[:, r, :].bitcast(E4M3), scales=scales[:, r, :], in_=dealt[:, r, :, :].rearrange("p s j -> p (s j)")
+            )
+
+        wd_b = tile("wd_b", [P, LANES, P, LANES], BF16)
+        deal(nc.scalar.copy, wd_b, wd_raw[0], 0)
+        deal(nc.vector.tensor_copy, wd_b, wd_raw[1], 1)
+        wd_q = tile("wd_q", [P, LANES, P], U32)
+        wd_s = tile("wd_s", [P, LANES, P], U8)
+        score = [ps.tile([P, N], F32, name="score%d" % r) for r in range(LANES)]
+        for r in range(LANES):
+            quantize_head(wd_b, wd_q, wd_s, r)
+            nc.tensor.matmul_mx(
+                out=score[r][:], lhsT=wd_q[:, r, :].bitcast(E4M3), lhsT_scale=wd_s[:, r, :],
+                rhs=x_q[:].bitcast(E4M3), rhs_scale=x_s[:], start=True, stop=True,
+            )
+
+        margin = [tile("margin%d" % r, [P, N], F32) for r in range(LANES)]
+        hinge = tile("hinge", [P, LANES, N], F32)
+        coef = tile("coef", [P, LANES, N], F32)
+        for r in range(LANES):
+            nc.vector.tensor_tensor(margin[r][:], score[r][:], y_sb[r][:], ALU.mult)
+            nc.scalar.activation(hinge[:, r, :], margin[r][:], ACT.Relu, bias=1.0, scale=-1.0)
+        for r in range(LANES):
+            nc.vector.scalar_tensor_tensor(coef[:, r, :], y_sb[r][:], neg_cw[:, r : r + 1], rw_sb[:], ALU.mult, ALU.mult)
+
+        wv_b = tile("wv_b", [P, LANES, P, LANES], BF16)
+        for h in range(2):
+            deal(nc.scalar.copy, wv_b, wv_raw[h], h)
+
+        g_b = tile("g_b", [P, N, LANES], BF16)
+        g_q_all = tile("g_q_all", [P, EARLY + N], U32)
+        g_s_all = tile("g_s_all", [P, EARLY + N], U8)
+        nc.vector.memset(g_q_all[:, :EARLY], 0)
+        nc.vector.memset(g_s_all[:, :EARLY].bitcast(U32), 0)
+        g_q = g_q_all[:, EARLY:]
+        g_s = g_s_all[:, EARLY:]
+
+        def g_round(c):
+            cols = slice(c * G_CHUNK, (c + 1) * G_CHUNK)
+            nc.vector.tensor_tensor(
+                g_b[:, cols, :].rearrange("p (c i) r -> p c r i", i=4),
+                hinge[:, :, cols].rearrange("p r (c i) -> p c r i", i=4),
+                coef[:, :, cols].rearrange("p r (c i) -> p c r i", i=4),
+                ALU.mult,
+            )
+
+        def g_quantize(c):
+            cols = slice(c * G_CHUNK, (c + 1) * G_CHUNK)
+            nc.vector.quantize_mx(out=g_q[:, cols].bitcast(E5M2), scales=g_s[:, cols], in_=g_b[:, cols, :].rearrange("p n r -> p (n r)"))
+
+        wv_q = tile("wv_q", [P, LANES, P], U32)
+        wv_s = tile("wv_s", [P, LANES, P], U8)
+        dx = [tile("dx%d" % t, [P, N], F32) for t in range(1, LANES)]
+        dx_first = [tile("dx_first%d" % h, [P, EARLY], F32) for h in range(2)]
+
+        def back(bank, t, cols):
+            nc.tensor.matmul_mx(
+                out=bank[:], lhsT=wv_q[:, t, :].bitcast(E4M3), lhsT_scale=wv_s[:, t, :],
+                rhs=g_q_all[:, cols].bitcast(E5M2), rhs_scale=g_s_all[:, cols], start=True, stop=True,
+            )
+
+        g_round(0)
+        g_round(1)
+        g_quantize(0)
+        quantize_head(wv_b, wv_q, wv_s, 0)
+        g_quantize(1)
+        early = ps.tile([P, N], F32, name="score0")
+        back(early, 0, slice(0, N))
+        nc.scalar.copy(dx_first[0][:], early[:, EARLY:])
+        g_round(2)
+        g_round(3)
+        g_quantize(2)
+        quantize_head(wv_b, wv_q, wv_s, 1)
+        g_quantize(3)
+        for t in range(2, LANES):
+            quantize_head(wv_b, wv_q, wv_s, t)
+
+        grad = [ps.tile([P, N], F32, name="grad%d" % t) for t in range(LANES)]
+        for t in range(LANES):
+            back(grad[t], t, slice(EARLY, EARLY + N))
+            if t == 0:
+                nc.scalar.copy(dx_first[1][:], grad[0][:, EARLY:])
+            else:
+                nc.scalar.copy(dx[t - 1][:], grad[t][:])
+
+        starts = [sum(OUT_CHUNKS[:c]) for c in range(len(OUT_CHUNKS))]
+        pairs = [tile("pairs%d" % c, [P, 2, n, 2], BF16) for c, n in enumerate(OUT_CHUNKS)]
+
+        def round_plane(t, c):
+            n = OUT_CHUNKS[c]
+            src = window[t][:, starts[c] : starts[c] + n]
+            if (t, c) == (LANES - 2, 0):
+                nc.scalar.copy(pairs[c][:, 1, :, :], src.unsqueeze(2).to_broadcast([P, n, 2]))
+            elif (t, c) == (LANES - 1, 0):
+                nc.vector.tensor_copy(pairs[c][:, 1, :, 1], src)
+            else:
+                nc.scalar.copy(pairs[c][:, t // 2, :, t % 2], src)
+
+        for t in range(LANES):
+            if t == 0:
+                for h in range(2):
+                    nc.vector.tensor_copy(window[0][:].indirect(offsets[:, h * EARLY // 16 : (h + 1) * EARLY // 16]), dx_first[h][:])
+            else:
+                nc.vector.tensor_copy(window[t][:].indirect(offsets[:]), dx[t - 1][:])
+            nc.sync.dma_start(out_rows[:, t, :], window[t][:])
+            for c in range(len(OUT_CHUNKS)):
+                round_plane(t, c)
+
+        out_words = out_1.rearrange("o p t l -> p (o t l)").bitcast(I32)
+        out_s = tile("out_s", [P, T], U8)
+        quads = [tile("quads%d" % c, [P, n, LANES], BF16) for c, n in enumerate(OUT_CHUNKS)]
+        out_q = [tile("out_q%d" % c, [P, n], U32) for c, n in enumerate(OUT_CHUNKS)]
+
+        def weave(c, copy, word):
+            n = OUT_CHUNKS[c]
+            copy(
+                quads[c][:].rearrange("p n l -> p (n l)").bitcast(word).rearrange("p (n u) -> p n u", u=2),
+                pairs[c][:].rearrange("p u n e -> p (u n e)").bitcast(word).rearrange("p (u n) -> p n u", n=n),
+            )
+
+        def out_quantize(c):
+            cols = slice(starts[c], starts[c] + OUT_CHUNKS[c])
+            nc.vector.quantize_mx(out=out_q[c][:].bitcast(E4M3), scales=out_s[:, cols], in_=quads[c][:].rearrange("p n l -> p (n l)"))
+            nc.sync.dma_start(out_words[:, cols], out_q[c][:].bitcast(I32))
+
+        weave(0, nc.vector.tensor_copy, I32)
+        weave(1, nc.vector.tensor_copy, I32)
+        out_quantize(0)
+        weave(2, nc.vector.tensor_copy, I32)
+        out_quantize(1)
+        weave(3, nc.scalar.copy, U32)
+        weave(4, nc.scalar.copy, U32)
+        for c in range(2, len(OUT_CHUNKS)):
+            out_quantize(c)
+        for q in range(4):
+            queue = nc.scalar if q % 2 else nc.sync
+            queue.dma_start(out_2[0, 4 * q : 4 * q + 4, :].bitcast(I32), out_s[32 * q : 32 * q + 4, :].bitcast(I32))

@@ -18,7 +18,8 @@ ACT = mybir.ActivationFunctionType
 
 P = 128
 LANES = 4
-G_CHUNK = 128
+G_CHUNK = 256
+WD_VECTOR_ROWS = 88
 OUT_CHUNKS = (512, 512, 512, 256, 256)
 EARLY = N // 2
 
@@ -29,15 +30,14 @@ def tile_attend_gml_pl_sqh_kernel(tc, xT, wd, wv, y, cw, rw, offs, out_0, out_1,
         sb = ctx.enter_context(tc.tile_pool(name="sb", bufs=1))
         ps = ctx.enter_context(tc.psum_pool(name="ps", bufs=1))
 
-        def tile(name, shape, dtype):
-            return sb.tile(shape, dtype, name=name, align_bytes=64)
+        def tile(name, shape, dtype, tag=None):
+            return sb.tile(shape, dtype, name=name, tag=tag or name, align_bytes=64)
 
         x_rows = xT.rearrange("(p j) t -> p j t", j=LANES)
         wd_rows = wd.rearrange("(p j) v -> p j v", j=LANES)
         wv_rows = wv.rearrange("(p j) d -> p j d", j=LANES)
         y_rows = y.rearrange("(p j) i -> p j i", j=LANES)
         out_rows = out_0.rearrange("(p j) t -> p j t", j=LANES)
-        half = V // 2
 
         offsets = sb.tile([P, N // 16], U16, name="offsets")
         nc.sync.dma_start(offsets[:], offs)
@@ -46,21 +46,21 @@ def tile_attend_gml_pl_sqh_kernel(tc, xT, wd, wv, y, cw, rw, offs, out_0, out_1,
         x_plane = [tile("x_plane%d" % j, [P, T], F32) for j in range(LANES)]
         for j in range(LANES):
             nc.sync.dma_start(x_plane[j][:], x_rows[:, j, :])
-        wd_raw = [tile("wd_raw%d" % h, [P, LANES, half], F32) for h in range(2)]
-        for h in range(2):
-            nc.sync.dma_start(wd_raw[h][:], wd_rows[:, :, h * half : (h + 1) * half])
+        wd_raw = tile("wd_raw", [P, LANES, V], F32)
+        nc.sync.dma_start(wd_raw[:], wd_rows)
         rw_sb = tile("rw_sb", [P, N], F32)
         nc.sync.dma_start(rw_sb[:], rw)
-        y_sb = [tile("y_sb%d" % r, [P, N], F32) for r in range(LANES)]
-        for r in range(LANES):
-            nc.sync.dma_start(y_sb[r][:], y_rows[:, r, :])
-        wv_raw = [tile("wv_raw%d" % h, [P, LANES, half], F32) for h in range(2)]
+        y_pair = [tile("y_pair%d" % h, [P, 2, N], F32) for h in range(2)]
         for h in range(2):
-            nc.sync.dma_start(wv_raw[h][:], wv_rows[:, :, h * half : (h + 1) * half])
+            nc.sync.dma_start(y_pair[h][:], y_rows[:, 2 * h : 2 * h + 2, :])
+        y_sb = [y_pair[r // 2][:, r % 2, :] for r in range(LANES)]
+        wv_raw = tile("wv_raw", [P, LANES, D], F32)
+        nc.sync.dma_start(wv_raw[:], wv_rows)
 
         window = [tile("window%d" % t, [P, T], F32) for t in range(LANES)]
-        for t in range(LANES):
+        for t in range(LANES - 1):
             nc.vector.memset(window[t][:], 0.0)
+        nc.gpsimd.memset(window[LANES - 1][:], 0.0)
         neg_cw = tile("neg_cw", [P, LANES], F32)
         nc.scalar.mul(neg_cw[:], cw_sb[:], -1.0)
 
@@ -71,9 +71,11 @@ def tile_attend_gml_pl_sqh_kernel(tc, xT, wd, wv, y, cw, rw, offs, out_0, out_1,
         x_s = tile("x_s", [P, N], U8)
         nc.vector.quantize_mx(out=x_q[:].bitcast(E4M3), scales=x_s[:], in_=x_b[:].rearrange("p n j -> p (n j)"))
 
-        def deal(copy, dealt, raw, h):
-            s_half = slice(h * P // 2, (h + 1) * P // 2)
-            copy(dealt[:, :, s_half, :].rearrange("p r s j -> p s j r"), raw[:].rearrange("p j (s r) -> p s j r", r=LANES))
+        def deal(copy, dealt, raw, s_range, r_range):
+            copy(
+                dealt[:, r_range, s_range, :].rearrange("p r s j -> p s j r"),
+                raw[:].rearrange("p j (s r) -> p s j r", r=LANES)[:, s_range, :, r_range],
+            )
 
         def quantize_head(dealt, codes, scales, r):
             nc.vector.quantize_mx(
@@ -81,8 +83,8 @@ def tile_attend_gml_pl_sqh_kernel(tc, xT, wd, wv, y, cw, rw, offs, out_0, out_1,
             )
 
         wd_b = tile("wd_b", [P, LANES, P, LANES], BF16)
-        deal(nc.scalar.copy, wd_b, wd_raw[0], 0)
-        deal(nc.vector.tensor_copy, wd_b, wd_raw[1], 1)
+        deal(nc.vector.tensor_copy, wd_b, wd_raw, slice(0, WD_VECTOR_ROWS), slice(0, LANES))
+        deal(nc.scalar.copy, wd_b, wd_raw, slice(WD_VECTOR_ROWS, P), slice(0, LANES))
         wd_q = tile("wd_q", [P, LANES, P], U32)
         wd_s = tile("wd_s", [P, LANES, P], U8)
         score = [ps.tile([P, N], F32, name="score%d" % r) for r in range(LANES)]
@@ -95,18 +97,22 @@ def tile_attend_gml_pl_sqh_kernel(tc, xT, wd, wv, y, cw, rw, offs, out_0, out_1,
 
         margin = [tile("margin%d" % r, [P, N], F32) for r in range(LANES)]
         hinge = tile("hinge", [P, LANES, N], F32)
-        coef = tile("coef", [P, LANES, N], F32)
+        coef = tile("coef", [P, LANES, N], F32, tag="wd_b")
+        weight = [tile("weight%d" % r, [P, N], F32) for r in range(2)]
+        for r in range(2):
+            nc.scalar.mul(weight[r][:], rw_sb[:], neg_cw[:, r : r + 1])
+            nc.gpsimd.tensor_tensor(coef[:, r, :], y_sb[r], weight[r][:], ALU.mult)
         for r in range(LANES):
-            nc.vector.tensor_tensor(margin[r][:], score[r][:], y_sb[r][:], ALU.mult)
+            nc.vector.tensor_tensor(margin[r][:], score[r][:], y_sb[r], ALU.mult)
             nc.scalar.activation(hinge[:, r, :], margin[r][:], ACT.Relu, bias=1.0, scale=-1.0)
-        for r in range(LANES):
-            nc.vector.scalar_tensor_tensor(coef[:, r, :], y_sb[r][:], neg_cw[:, r : r + 1], rw_sb[:], ALU.mult, ALU.mult)
+        for r in range(2, LANES):
+            nc.vector.scalar_tensor_tensor(coef[:, r, :], y_sb[r], neg_cw[:, r : r + 1], rw_sb[:], ALU.mult, ALU.mult)
 
         wv_b = tile("wv_b", [P, LANES, P, LANES], BF16)
         for h in range(2):
-            deal(nc.scalar.copy, wv_b, wv_raw[h], h)
+            deal(nc.scalar.copy, wv_b, wv_raw, slice(0, P), slice(2 * h, 2 * h + 2))
 
-        g_b = tile("g_b", [P, N, LANES], BF16)
+        g_b = {}
         g_q_all = tile("g_q_all", [P, EARLY + N], U32)
         g_s_all = tile("g_s_all", [P, EARLY + N], U8)
         nc.vector.memset(g_q_all[:, :EARLY], 0)
@@ -116,8 +122,9 @@ def tile_attend_gml_pl_sqh_kernel(tc, xT, wd, wv, y, cw, rw, offs, out_0, out_1,
 
         def g_round(c):
             cols = slice(c * G_CHUNK, (c + 1) * G_CHUNK)
+            g_b[c] = tile("g_b%d" % c, [P, G_CHUNK, LANES], BF16, tag="g_b")
             nc.vector.tensor_tensor(
-                g_b[:, cols, :].rearrange("p (c i) r -> p c r i", i=4),
+                g_b[c][:].rearrange("p (c i) r -> p c r i", i=4),
                 hinge[:, :, cols].rearrange("p r (c i) -> p c r i", i=4),
                 coef[:, :, cols].rearrange("p r (c i) -> p c r i", i=4),
                 ALU.mult,
@@ -125,7 +132,7 @@ def tile_attend_gml_pl_sqh_kernel(tc, xT, wd, wv, y, cw, rw, offs, out_0, out_1,
 
         def g_quantize(c):
             cols = slice(c * G_CHUNK, (c + 1) * G_CHUNK)
-            nc.vector.quantize_mx(out=g_q[:, cols].bitcast(E5M2), scales=g_s[:, cols], in_=g_b[:, cols, :].rearrange("p n r -> p (n r)"))
+            nc.vector.quantize_mx(out=g_q[:, cols].bitcast(E5M2), scales=g_s[:, cols], in_=g_b[c][:].rearrange("p n r -> p (n r)"))
 
         wv_q = tile("wv_q", [P, LANES, P], U32)
         wv_s = tile("wv_s", [P, LANES, P], U8)
@@ -138,19 +145,19 @@ def tile_attend_gml_pl_sqh_kernel(tc, xT, wd, wv, y, cw, rw, offs, out_0, out_1,
                 rhs=g_q_all[:, cols].bitcast(E5M2), rhs_scale=g_s_all[:, cols], start=True, stop=True,
             )
 
+        def scatter_first(h):
+            nc.vector.tensor_copy(window[0][:].indirect(offsets[:, h * EARLY // 16 : (h + 1) * EARLY // 16]), dx_first[h][:])
+
         g_round(0)
-        g_round(1)
-        g_quantize(0)
         quantize_head(wv_b, wv_q, wv_s, 0)
-        g_quantize(1)
+        g_quantize(0)
         early = ps.tile([P, N], F32, name="score0")
         back(early, 0, slice(0, N))
         nc.scalar.copy(dx_first[0][:], early[:, EARLY:])
-        g_round(2)
-        g_round(3)
-        g_quantize(2)
+        g_round(1)
         quantize_head(wv_b, wv_q, wv_s, 1)
-        g_quantize(3)
+        g_quantize(1)
+        scatter_first(0)
         for t in range(2, LANES):
             quantize_head(wv_b, wv_q, wv_s, t)
 
@@ -177,8 +184,7 @@ def tile_attend_gml_pl_sqh_kernel(tc, xT, wd, wv, y, cw, rw, offs, out_0, out_1,
 
         for t in range(LANES):
             if t == 0:
-                for h in range(2):
-                    nc.vector.tensor_copy(window[0][:].indirect(offsets[:, h * EARLY // 16 : (h + 1) * EARLY // 16]), dx_first[h][:])
+                scatter_first(1)
             else:
                 nc.vector.tensor_copy(window[t][:].indirect(offsets[:]), dx[t - 1][:])
             nc.sync.dma_start(out_rows[:, t, :], window[t][:])

@@ -1,6 +1,7 @@
 from contextlib import ExitStack
 
 import concourse.mybir as mybir
+from concourse.masks import make_identity
 
 N, T, D, V = 512, 2048, 512, 512
 FLOPS = 2 * 2 * D * V * N
@@ -19,7 +20,6 @@ ACT = mybir.ActivationFunctionType
 P = 128
 LANES = 4
 G_CHUNK = 256
-WD_VECTOR_ROWS = 88
 OUT_CHUNKS = (512, 512, 512, 256, 256)
 EARLY = N // 2
 
@@ -43,13 +43,13 @@ def tile_attend_gml_pl_sqh_kernel(tc, xT, wd, wv, y, cw, rw, offs, out_0, out_1,
         nc.sync.dma_start(offsets[:], offs)
         cw_sb = tile("cw_sb", [P, LANES], F32)
         nc.scalar.dma_start(cw_sb[:], cw.rearrange("(p j) o -> p (j o)", j=LANES))
+        rw_sb = tile("rw_sb", [P, LANES], F32)
+        nc.scalar.dma_start(rw_sb[:], rw[0:1, :].rearrange("o (p c) -> p (o c)", c=LANES))
         x_plane = [tile("x_plane%d" % j, [P, T], F32) for j in range(LANES)]
         for j in range(LANES):
             nc.sync.dma_start(x_plane[j][:], x_rows[:, j, :])
         wd_raw = tile("wd_raw", [P, LANES, V], F32)
         nc.sync.dma_start(wd_raw[:], wd_rows)
-        rw_sb = tile("rw_sb", [P, N], F32)
-        nc.sync.dma_start(rw_sb[:], rw)
         y_pair = [tile("y_pair%d" % h, [P, 2, N], F32) for h in range(2)]
         for h in range(2):
             nc.sync.dma_start(y_pair[h][:], y_rows[:, 2 * h : 2 * h + 2, :])
@@ -58,11 +58,19 @@ def tile_attend_gml_pl_sqh_kernel(tc, xT, wd, wv, y, cw, rw, offs, out_0, out_1,
         nc.sync.dma_start(wv_raw[:], wv_rows)
 
         window = [tile("window%d" % t, [P, T], F32) for t in range(LANES)]
-        for t in range(LANES - 1):
+        for t in range(LANES):
             nc.vector.memset(window[t][:], 0.0)
-        nc.gpsimd.memset(window[LANES - 1][:], 0.0)
         neg_cw = tile("neg_cw", [P, LANES], F32)
         nc.scalar.mul(neg_cw[:], cw_sb[:], -1.0)
+
+        ident = tile("ident", [P, P], F32)
+        make_identity(nc, ident[:])
+        rw_all = ps.tile([P, LANES, P], F32, name="grad3")
+        for c in range(LANES):
+            nc.tensor.transpose(rw_all[:, c, :], rw_sb[:, c : c + 1].to_broadcast([P, P]), ident[:])
+        weight = tile("weight", [P, LANES, N], F32)
+        for r in range(LANES):
+            nc.scalar.mul(weight[:, r, :].rearrange("m (p c) -> m p c", c=LANES), rw_all[:].rearrange("m c p -> m p c"), neg_cw[:, r : r + 1])
 
         x_b = tile("x_b", [P, N, LANES], BF16)
         for j in range(LANES):
@@ -83,8 +91,8 @@ def tile_attend_gml_pl_sqh_kernel(tc, xT, wd, wv, y, cw, rw, offs, out_0, out_1,
             )
 
         wd_b = tile("wd_b", [P, LANES, P, LANES], BF16)
-        deal(nc.vector.tensor_copy, wd_b, wd_raw, slice(0, WD_VECTOR_ROWS), slice(0, LANES))
-        deal(nc.scalar.copy, wd_b, wd_raw, slice(WD_VECTOR_ROWS, P), slice(0, LANES))
+        deal(nc.vector.tensor_copy, wd_b, wd_raw, slice(0, P), slice(0, 2))
+        deal(nc.scalar.copy, wd_b, wd_raw, slice(0, P), slice(2, LANES))
         wd_q = tile("wd_q", [P, LANES, P], U32)
         wd_s = tile("wd_s", [P, LANES, P], U8)
         score = [ps.tile([P, N], F32, name="score%d" % r) for r in range(LANES)]
@@ -97,16 +105,12 @@ def tile_attend_gml_pl_sqh_kernel(tc, xT, wd, wv, y, cw, rw, offs, out_0, out_1,
 
         margin = [tile("margin%d" % r, [P, N], F32) for r in range(LANES)]
         hinge = tile("hinge", [P, LANES, N], F32)
-        coef = tile("coef", [P, LANES, N], F32, tag="wd_b")
-        weight = [tile("weight%d" % r, [P, N], F32) for r in range(2)]
-        for r in range(2):
-            nc.scalar.mul(weight[r][:], rw_sb[:], neg_cw[:, r : r + 1])
-            nc.gpsimd.tensor_tensor(coef[:, r, :], y_sb[r], weight[r][:], ALU.mult)
+        coef = tile("coef", [P, LANES, N], F32)
         for r in range(LANES):
             nc.vector.tensor_tensor(margin[r][:], score[r][:], y_sb[r], ALU.mult)
             nc.scalar.activation(hinge[:, r, :], margin[r][:], ACT.Relu, bias=1.0, scale=-1.0)
-        for r in range(2, LANES):
-            nc.vector.scalar_tensor_tensor(coef[:, r, :], y_sb[r], neg_cw[:, r : r + 1], rw_sb[:], ALU.mult, ALU.mult)
+        for h in range(2):
+            nc.vector.tensor_tensor(coef[:, 2 * h : 2 * h + 2, :], y_pair[h][:], weight[:, 2 * h : 2 * h + 2, :], ALU.mult)
 
         wv_b = tile("wv_b", [P, LANES, P, LANES], BF16)
         for h in range(2):
@@ -124,9 +128,9 @@ def tile_attend_gml_pl_sqh_kernel(tc, xT, wd, wv, y, cw, rw, offs, out_0, out_1,
             cols = slice(c * G_CHUNK, (c + 1) * G_CHUNK)
             g_b[c] = tile("g_b%d" % c, [P, G_CHUNK, LANES], BF16, tag="g_b")
             nc.vector.tensor_tensor(
-                g_b[c][:].rearrange("p (c i) r -> p c r i", i=4),
-                hinge[:, :, cols].rearrange("p r (c i) -> p c r i", i=4),
-                coef[:, :, cols].rearrange("p r (c i) -> p c r i", i=4),
+                g_b[c][:].rearrange("p (c i) r -> p c r i", i=2),
+                hinge[:, :, cols].rearrange("p r (c i) -> p c r i", i=2),
+                coef[:, :, cols].rearrange("p r (c i) -> p c r i", i=2),
                 ALU.mult,
             )
 
@@ -157,9 +161,9 @@ def tile_attend_gml_pl_sqh_kernel(tc, xT, wd, wv, y, cw, rw, offs, out_0, out_1,
         g_round(1)
         quantize_head(wv_b, wv_q, wv_s, 1)
         g_quantize(1)
-        scatter_first(0)
         for t in range(2, LANES):
             quantize_head(wv_b, wv_q, wv_s, t)
+        scatter_first(0)
 
         grad = [ps.tile([P, N], F32, name="grad%d" % t) for t in range(LANES)]
         for t in range(LANES):
@@ -197,10 +201,9 @@ def tile_attend_gml_pl_sqh_kernel(tc, xT, wd, wv, y, cw, rw, offs, out_0, out_1,
         out_q = [tile("out_q%d" % c, [P, n], U32) for c, n in enumerate(OUT_CHUNKS)]
 
         def weave(c, copy, word):
-            n = OUT_CHUNKS[c]
             copy(
-                quads[c][:].rearrange("p n l -> p (n l)").bitcast(word).rearrange("p (n u) -> p n u", u=2),
-                pairs[c][:].rearrange("p u n e -> p (u n e)").bitcast(word).rearrange("p (u n) -> p n u", n=n),
+                quads[c][:].rearrange("p n l -> p (n l)").bitcast(word).rearrange("p (c i u) -> p c u i", i=2, u=2),
+                pairs[c][:].rearrange("p u n e -> p (u n e)").bitcast(word).rearrange("p (u c i) -> p c u i", u=2, i=2),
             )
 
         def out_quantize(c):

@@ -20,7 +20,8 @@ ACT = mybir.ActivationFunctionType
 P = 128
 LANES = 4
 G_CHUNK = 256
-OUT_CHUNKS = (512, 512, 512, 256, 256)
+OUT_CHUNKS = (512, 512, 256, 512, 256)
+GPSIMD_FROM = 2
 EARLY = N // 2
 
 
@@ -179,8 +180,10 @@ def tile_attend_gml_pl_sqh_kernel(tc, xT, wd, wv, y, cw, rw, offs, out_0, out_1,
         def round_plane(t, c):
             n = OUT_CHUNKS[c]
             src = window[t][:, starts[c] : starts[c] + n]
-            if (t, c) == (LANES - 2, 0):
-                nc.scalar.copy(pairs[c][:, 1, :, :], src.unsqueeze(2).to_broadcast([P, n, 2]))
+            if t < 2 and c >= GPSIMD_FROM:
+                nc.gpsimd.tensor_scalar(pairs[c][:, 0, :, t], src, 1.0, -0.0, ALU.mult, ALU.add)
+            elif (t, c) == (LANES - 2, 0):
+                nc.gpsimd.tensor_scalar(pairs[c][:, 1, :, :], src.unsqueeze(2).to_broadcast([P, n, 2]), 1.0, -0.0, ALU.mult, ALU.add)
             elif (t, c) == (LANES - 1, 0):
                 nc.vector.tensor_copy(pairs[c][:, 1, :, 1], src)
             else:
@@ -191,7 +194,7 @@ def tile_attend_gml_pl_sqh_kernel(tc, xT, wd, wv, y, cw, rw, offs, out_0, out_1,
                 scatter_first(1)
             else:
                 nc.vector.tensor_copy(window[t][:].indirect(offsets[:]), dx[t - 1][:])
-            nc.sync.dma_start(out_rows[:, t, :], window[t][:])
+            (nc.scalar if t == LANES - 1 else nc.sync).dma_start(out_rows[:, t, :], window[t][:])
             for c in range(len(OUT_CHUNKS)):
                 round_plane(t, c)
 

@@ -51,9 +51,10 @@ def tile_attend_gml_pl_sqh_kernel(tc, xT, wd, wv, y, cw, rw, offs, out_0, out_1,
             nc.sync.dma_start(x_plane[j][:], x_rows[:, j, :])
         wd_raw = tile("wd_raw", [P, LANES, V], F32)
         nc.sync.dma_start(wd_raw[:], wd_rows)
-        y_pair = [tile("y_pair%d" % h, [P, 2, N], F32) for h in range(2)]
+        y_all = tile("y_all", [P, 6, N], F32)
+        y_pair = [y_all[:, 4 * h : 4 * h + 2, :] for h in range(2)]
         for h in range(2):
-            nc.sync.dma_start(y_pair[h][:], y_rows[:, 2 * h : 2 * h + 2, :])
+            nc.sync.dma_start(y_pair[h], y_rows[:, 2 * h : 2 * h + 2, :])
         y_sb = [y_pair[r // 2][:, r % 2, :] for r in range(LANES)]
         wv_raw = tile("wv_raw", [P, LANES, D], F32)
         nc.sync.dma_start(wv_raw[:], wv_rows)
@@ -66,6 +67,8 @@ def tile_attend_gml_pl_sqh_kernel(tc, xT, wd, wv, y, cw, rw, offs, out_0, out_1,
 
         ident = tile("ident", [P, P], F32)
         make_identity(nc, ident[:])
+        warm = tile("warm", [P, 8], F32)
+        nc.gpsimd.tensor_tensor(warm[:], ident[:, 0:8], ident[:, 8:16], ALU.mult)
         rw_all = ps.tile([P, LANES, P], F32, name="grad3")
         for c in range(LANES):
             nc.tensor.transpose(rw_all[:, c, :], rw_sb[:, c : c + 1].to_broadcast([P, P]), ident[:])
@@ -106,12 +109,14 @@ def tile_attend_gml_pl_sqh_kernel(tc, xT, wd, wv, y, cw, rw, offs, out_0, out_1,
 
         margin = [tile("margin%d" % r, [P, N], F32) for r in range(LANES)]
         hinge = tile("hinge", [P, LANES, N], F32)
-        coef = tile("coef", [P, LANES, N], F32)
-        for r in range(LANES):
-            nc.vector.tensor_tensor(margin[r][:], score[r][:], y_sb[r], ALU.mult)
-            nc.scalar.activation(hinge[:, r, :], margin[r][:], ACT.Relu, bias=1.0, scale=-1.0)
+        coef = [tile("coef0", [P, LANES, G_CHUNK], F32, tag="wd_b")[:], y_all[:, 2:, G_CHUNK:]]
+        nc.vector.tensor_tensor(coef[1][:, :2, :], y_pair[0][:, :, G_CHUNK:], weight[:, :2, G_CHUNK:], ALU.mult)
         for h in range(2):
-            nc.vector.tensor_tensor(coef[:, 2 * h : 2 * h + 2, :], y_pair[h][:], weight[:, 2 * h : 2 * h + 2, :], ALU.mult)
+            nc.gpsimd.tensor_tensor(coef[0][:, 2 * h : 2 * h + 2, :], y_pair[h][:, :, :G_CHUNK], weight[:, 2 * h : 2 * h + 2, :G_CHUNK], ALU.mult)
+        for r in range(LANES):
+            nc.vector.tensor_tensor(margin[r][:], y_sb[r], score[r][:], ALU.mult)
+            nc.scalar.activation(hinge[:, r, :], margin[r][:], ACT.Relu, bias=1.0, scale=-1.0)
+        nc.vector.tensor_tensor(coef[1][:, 2:, :], y_pair[1][:, :, G_CHUNK:], weight[:, 2:, G_CHUNK:], ALU.mult)
 
         wv_b = tile("wv_b", [P, LANES, P, LANES], BF16)
         for h in range(2):
@@ -131,7 +136,7 @@ def tile_attend_gml_pl_sqh_kernel(tc, xT, wd, wv, y, cw, rw, offs, out_0, out_1,
             nc.vector.tensor_tensor(
                 g_b[c][:].rearrange("p (c i) r -> p c r i", i=2),
                 hinge[:, :, cols].rearrange("p r (c i) -> p c r i", i=2),
-                coef[:, :, cols].rearrange("p r (c i) -> p c r i", i=2),
+                coef[c].rearrange("p r (c i) -> p c r i", i=2),
                 ALU.mult,
             )
 

@@ -62,13 +62,13 @@ def tile_attend_gml_pl_sqh_kernel(tc, xT, wd, wv, y, cw, rw, offs, out_0, out_1,
         window = [tile("window%d" % t, [P, T], F32) for t in range(LANES)]
         for t in range(LANES):
             nc.vector.memset(window[t][:], 0.0)
-        neg_cw = tile("neg_cw", [P, LANES], F32)
-        nc.scalar.mul(neg_cw[:], cw_sb[:], -1.0)
 
         ident = tile("ident", [P, P], F32)
         make_identity(nc, ident[:])
-        warm = tile("warm", [P, 8], F32)
-        nc.gpsimd.tensor_tensor(warm[:], ident[:, 0:8], ident[:, 8:16], ALU.mult)
+        minus_one = tile("minus_one", [P, LANES], F32)
+        nc.gpsimd.memset(minus_one[:], -1.0)
+        neg_cw = tile("neg_cw", [P, LANES], F32)
+        nc.gpsimd.tensor_tensor(neg_cw[:], cw_sb[:], minus_one[:], ALU.mult)
         rw_all = ps.tile([P, LANES, P], F32, name="grad3")
         for c in range(LANES):
             nc.tensor.transpose(rw_all[:, c, :], rw_sb[:, c : c + 1].to_broadcast([P, P]), ident[:])
@@ -130,24 +130,22 @@ def tile_attend_gml_pl_sqh_kernel(tc, xT, wd, wv, y, cw, rw, offs, out_0, out_1,
         g_q = g_q_all[:, EARLY:]
         g_s = g_s_all[:, EARLY:]
 
-        def g_round(c):
-            cols = slice(c * G_CHUNK, (c + 1) * G_CHUNK)
-            g_b[c] = tile("g_b%d" % c, [P, G_CHUNK, LANES], BF16, tag="g_b")
-            nc.vector.tensor_tensor(
-                g_b[c][:].rearrange("p (c i) r -> p c r i", i=2),
-                hinge[:, :, cols].rearrange("p r (c i) -> p c r i", i=2),
-                coef[c].rearrange("p r (c i) -> p c r i", i=2),
+        def g_round(engine, first, n):
+            half, at = divmod(first, G_CHUNK)
+            g_b[first] = tile("g_b%d" % first, [P, n, LANES], BF16, tag="g_b")
+            engine.tensor_tensor(
+                g_b[first][:].rearrange("p (c i) r -> p c r i", i=2),
+                hinge[:, :, first : first + n].rearrange("p r (c i) -> p c r i", i=2),
+                coef[half][:, :, at : at + n].rearrange("p r (c i) -> p c r i", i=2),
                 ALU.mult,
             )
 
-        def g_quantize(c):
-            cols = slice(c * G_CHUNK, (c + 1) * G_CHUNK)
-            nc.vector.quantize_mx(out=g_q[:, cols].bitcast(E5M2), scales=g_s[:, cols], in_=g_b[c][:].rearrange("p n r -> p (n r)"))
+        def g_quantize(first, n):
+            cols = slice(first, first + n)
+            nc.vector.quantize_mx(out=g_q[:, cols].bitcast(E5M2), scales=g_s[:, cols], in_=g_b[first][:].rearrange("p n r -> p (n r)"))
 
         wv_q = tile("wv_q", [P, LANES, P], U32)
         wv_s = tile("wv_s", [P, LANES, P], U8)
-        dx = [tile("dx%d" % t, [P, N], F32) for t in range(1, LANES)]
-        dx_first = [tile("dx_first%d" % h, [P, EARLY], F32) for h in range(2)]
 
         def back(bank, t, cols):
             nc.tensor.matmul_mx(
@@ -155,29 +153,46 @@ def tile_attend_gml_pl_sqh_kernel(tc, xT, wd, wv, y, cw, rw, offs, out_0, out_1,
                 rhs=g_q_all[:, cols].bitcast(E5M2), rhs_scale=g_s_all[:, cols], start=True, stop=True,
             )
 
-        def scatter_first(h):
-            nc.vector.tensor_copy(window[0][:].indirect(offsets[:, h * EARLY // 16 : (h + 1) * EARLY // 16]), dx_first[h][:])
+        dx_half = {(t, h): tile("dx_half%d%d" % (t, h), [P, EARLY], F32) for t, h in ((0, 0), (0, 1), (1, 1))}
+        early = {}
+        dx = {t: tile("dx%d" % t, [P, N], F32) for t in range(2, LANES)}
 
-        g_round(0)
+        def scatter_half(t, h):
+            nc.vector.tensor_copy(window[t][:].indirect(offsets[:, h * EARLY // 16 : (h + 1) * EARLY // 16]), dx_half[t, h][:])
+
+        def early_pass(t):
+            early[t] = ps.tile([P, N], F32, name="score%d" % t)
+            back(early[t], t, slice(0, N))
+
+        quarter = N // 4
+        g_round(nc.vector, 0, EARLY)
         quantize_head(wv_b, wv_q, wv_s, 0)
-        g_quantize(0)
-        early = ps.tile([P, N], F32, name="score0")
-        back(early, 0, slice(0, N))
-        nc.scalar.copy(dx_first[0][:], early[:, EARLY:])
-        g_round(1)
+        g_quantize(0, EARLY)
+        early_pass(0)
+        nc.scalar.copy(dx_half[0, 0][:], early[0][:, EARLY:])
+        g_round(nc.vector, EARLY, quarter)
         quantize_head(wv_b, wv_q, wv_s, 1)
-        g_quantize(1)
-        for t in range(2, LANES):
-            quantize_head(wv_b, wv_q, wv_s, t)
-        scatter_first(0)
+        early_pass(1)
+        nc.vector.quantize_mx(
+            out=wv_q[:, 2:, :].rearrange("p r s -> p (r s)").bitcast(E4M3),
+            scales=wv_s[:, 2:, :].rearrange("p r s -> p (r s)"),
+            in_=wv_b[:, 2:, :, :].rearrange("p r s j -> p (r s j)"),
+        )
+        g_quantize(EARLY, quarter)
+        g_round(nc.gpsimd, EARLY + quarter, quarter)
+        dx_half[1, 0] = tile("dx_half10", [P, EARLY], F32, tag="hinge")
+        nc.scalar.copy(dx_half[1, 0][:], early[1][:, EARLY:])
+        scatter_half(0, 0)
+        g_quantize(EARLY + quarter, quarter)
+        scatter_half(1, 0)
 
         grad = [ps.tile([P, N], F32, name="grad%d" % t) for t in range(LANES)]
         for t in range(LANES):
             back(grad[t], t, slice(EARLY, EARLY + N))
-            if t == 0:
-                nc.scalar.copy(dx_first[1][:], grad[0][:, EARLY:])
+            if t < 2:
+                nc.scalar.copy(dx_half[t, 1][:], grad[t][:, EARLY:])
             else:
-                nc.scalar.copy(dx[t - 1][:], grad[t][:])
+                nc.scalar.copy(dx[t][:], grad[t][:])
 
         starts = [sum(OUT_CHUNKS[:c]) for c in range(len(OUT_CHUNKS))]
         pairs = [tile("pairs%d" % c, [P, 2, n, 2], BF16) for c, n in enumerate(OUT_CHUNKS)]
@@ -195,10 +210,10 @@ def tile_attend_gml_pl_sqh_kernel(tc, xT, wd, wv, y, cw, rw, offs, out_0, out_1,
                 nc.scalar.copy(pairs[c][:, t // 2, :, t % 2], src)
 
         for t in range(LANES):
-            if t == 0:
-                scatter_first(1)
+            if t < 2:
+                scatter_half(t, 1)
             else:
-                nc.vector.tensor_copy(window[t][:].indirect(offsets[:]), dx[t - 1][:])
+                nc.vector.tensor_copy(window[t][:].indirect(offsets[:]), dx[t][:])
             (nc.scalar if t == LANES - 1 else nc.sync).dma_start(out_rows[:, t, :], window[t][:])
             for c in range(len(OUT_CHUNKS)):
                 round_plane(t, c)

@@ -134,9 +134,9 @@ def tile_attend_gml_pl_sqh_kernel(tc, xT, wd, wv, y, cw, rw, offs, out_0, out_1,
             half, at = divmod(first, G_CHUNK)
             g_b[first] = tile("g_b%d" % first, [P, n, LANES], BF16, tag="g_b")
             engine.tensor_tensor(
-                g_b[first][:].rearrange("p (c i) r -> p c r i", i=2),
-                hinge[:, :, first : first + n].rearrange("p r (c i) -> p c r i", i=2),
-                coef[half][:, :, at : at + n].rearrange("p r (c i) -> p c r i", i=2),
+                g_b[first][:].rearrange("p (c i) r -> p c r i", i=4),
+                hinge[:, :, first : first + n].rearrange("p r (c i) -> p c r i", i=4),
+                coef[half][:, :, at : at + n].rearrange("p r (c i) -> p c r i", i=4),
                 ALU.mult,
             )
 

@@ -20,9 +20,8 @@ ACT = mybir.ActivationFunctionType
 P = 128
 LANES = 4
 G_CHUNK = 256
-OUT_CHUNKS = (512, 512, 256, 512, 256)
-GPSIMD_FROM = 2
-EARLY = N // 2
+OUT_CHUNKS = (512, 512, 256, 256, 512)
+HALF = N // 2
 
 
 def tile_attend_gml_pl_sqh_kernel(tc, xT, wd, wv, y, cw, rw, offs, out_0, out_1, out_2):
@@ -122,101 +121,97 @@ def tile_attend_gml_pl_sqh_kernel(tc, xT, wd, wv, y, cw, rw, offs, out_0, out_1,
         for h in range(2):
             deal(nc.scalar.copy, wv_b, wv_raw, slice(0, P), slice(2 * h, 2 * h + 2))
 
-        g_b = {}
-        g_q_all = tile("g_q_all", [P, EARLY + N], U32)
-        g_s_all = tile("g_s_all", [P, EARLY + N], U8)
-        nc.vector.memset(g_q_all[:, :EARLY], 0)
-        nc.vector.memset(g_s_all[:, :EARLY].bitcast(U32), 0)
-        g_q = g_q_all[:, EARLY:]
-        g_s = g_s_all[:, EARLY:]
+        g_q = tile("g_q", [P, N], U32)
+        g_s = tile("g_s", [P, N], U8)
+        g_b = [tile("g_b%d" % h, [P, HALF, LANES], BF16) for h in range(2)]
+        halves = [slice(h * HALF, (h + 1) * HALF) for h in range(2)]
 
-        def g_round(engine, first, n):
-            half, at = divmod(first, G_CHUNK)
-            g_b[first] = tile("g_b%d" % first, [P, n, LANES], BF16, tag="g_b")
-            engine.tensor_tensor(
-                g_b[first][:].rearrange("p (c i) r -> p c r i", i=4),
-                hinge[:, :, first : first + n].rearrange("p r (c i) -> p c r i", i=4),
-                coef[half][:, :, at : at + n].rearrange("p r (c i) -> p c r i", i=4),
+        def g_round(h):
+            nc.vector.tensor_tensor(
+                g_b[h][:].rearrange("p (c i) r -> p c r i", i=4),
+                hinge[:, :, halves[h]].rearrange("p r (c i) -> p c r i", i=4),
+                coef[h].rearrange("p r (c i) -> p c r i", i=4),
                 ALU.mult,
             )
 
-        def g_quantize(first, n):
-            cols = slice(first, first + n)
-            nc.vector.quantize_mx(out=g_q[:, cols].bitcast(E5M2), scales=g_s[:, cols], in_=g_b[first][:].rearrange("p n r -> p (n r)"))
+        def g_quantize(h):
+            nc.vector.quantize_mx(out=g_q[:, halves[h]].bitcast(E5M2), scales=g_s[:, halves[h]], in_=g_b[h][:].rearrange("p n r -> p (n r)"))
 
         wv_q = tile("wv_q", [P, LANES, P], U32)
         wv_s = tile("wv_s", [P, LANES, P], U8)
 
-        def back(bank, t, cols):
-            nc.tensor.matmul_mx(
-                out=bank[:], lhsT=wv_q[:, t, :].bitcast(E4M3), lhsT_scale=wv_s[:, t, :],
-                rhs=g_q_all[:, cols].bitcast(E5M2), rhs_scale=g_s_all[:, cols], start=True, stop=True,
+        def quantize_wv(h):
+            rows = slice(2 * h, 2 * h + 2)
+            nc.vector.quantize_mx(
+                out=wv_q[:, rows, :].rearrange("p r s -> p (r s)").bitcast(E4M3),
+                scales=wv_s[:, rows, :].rearrange("p r s -> p (r s)"),
+                in_=wv_b[:, rows, :, :].rearrange("p r s j -> p (r s j)"),
             )
 
-        dx_half = {(t, h): tile("dx_half%d%d" % (t, h), [P, EARLY], F32) for t, h in ((0, 0), (0, 1), (1, 1))}
-        early = {}
-        dx = {t: tile("dx%d" % t, [P, N], F32) for t in range(2, LANES)}
+        def back(bank, t, cols):
+            nc.tensor.matmul_mx(
+                out=bank, lhsT=wv_q[:, t, :].bitcast(E4M3), lhsT_scale=wv_s[:, t, :],
+                rhs=g_q[:, cols].bitcast(E5M2), rhs_scale=g_s[:, cols], start=True, stop=True,
+            )
 
-        def scatter_half(t, h):
-            nc.vector.tensor_copy(window[t][:].indirect(offsets[:, h * EARLY // 16 : (h + 1) * EARLY // 16]), dx_half[t, h][:])
+        def listed(t, h):
+            return window[t][:].indirect(offsets[:, h * HALF // 16 : (h + 1) * HALF // 16])
 
-        def early_pass(t):
-            early[t] = ps.tile([P, N], F32, name="score%d" % t)
-            back(early[t], t, slice(0, N))
-
-        quarter = N // 4
-        g_round(nc.vector, 0, EARLY)
-        quantize_head(wv_b, wv_q, wv_s, 0)
-        g_quantize(0, EARLY)
-        early_pass(0)
-        nc.scalar.copy(dx_half[0, 0][:], early[0][:, EARLY:])
-        g_round(nc.vector, EARLY, quarter)
-        quantize_head(wv_b, wv_q, wv_s, 1)
-        early_pass(1)
-        nc.vector.quantize_mx(
-            out=wv_q[:, 2:, :].rearrange("p r s -> p (r s)").bitcast(E4M3),
-            scales=wv_s[:, 2:, :].rearrange("p r s -> p (r s)"),
-            in_=wv_b[:, 2:, :, :].rearrange("p r s j -> p (r s j)"),
-        )
-        g_quantize(EARLY, quarter)
-        g_round(nc.gpsimd, EARLY + quarter, quarter)
-        dx_half[1, 0] = tile("dx_half10", [P, EARLY], F32, tag="hinge")
-        nc.scalar.copy(dx_half[1, 0][:], early[1][:, EARLY:])
-        scatter_half(0, 0)
-        g_quantize(EARLY + quarter, quarter)
-        scatter_half(1, 0)
-
-        grad = [ps.tile([P, N], F32, name="grad%d" % t) for t in range(LANES)]
-        for t in range(LANES):
-            back(grad[t], t, slice(EARLY, EARLY + N))
-            if t < 2:
-                nc.scalar.copy(dx_half[t, 1][:], grad[t][:, EARLY:])
-            else:
-                nc.scalar.copy(dx[t][:], grad[t][:])
+        def store_plane(t):
+            (nc.scalar if t == 2 else nc.sync).dma_start(out_rows[:, t, :], window[t][:])
 
         starts = [sum(OUT_CHUNKS[:c]) for c in range(len(OUT_CHUNKS))]
         pairs = [tile("pairs%d" % c, [P, 2, n, 2], BF16) for c, n in enumerate(OUT_CHUNKS)]
 
-        def round_plane(t, c):
-            n = OUT_CHUNKS[c]
-            src = window[t][:, starts[c] : starts[c] + n]
-            if t < 2 and c >= GPSIMD_FROM:
-                nc.gpsimd.tensor_scalar(pairs[c][:, 0, :, t], src, 1.0, -0.0, ALU.mult, ALU.add)
-            elif (t, c) == (LANES - 2, 0):
-                nc.gpsimd.tensor_scalar(pairs[c][:, 1, :, :], src.unsqueeze(2).to_broadcast([P, n, 2]), 1.0, -0.0, ALU.mult, ALU.add)
-            elif (t, c) == (LANES - 1, 0):
-                nc.vector.tensor_copy(pairs[c][:, 1, :, 1], src)
+        def round_plane(engine, t, c):
+            src = window[t][:, starts[c] : starts[c] + OUT_CHUNKS[c]]
+            dst = pairs[c][:, t // 2, :, t % 2]
+            if engine == "gpsimd":
+                nc.gpsimd.tensor_scalar(dst, src, 1.0, -0.0, ALU.mult, ALU.add)
+            elif engine == "vector":
+                nc.vector.tensor_copy(dst, src)
             else:
-                nc.scalar.copy(pairs[c][:, t // 2, :, t % 2], src)
+                nc.scalar.copy(dst, src)
 
-        for t in range(LANES):
-            if t < 2:
-                scatter_half(t, 1)
-            else:
-                nc.vector.tensor_copy(window[t][:].indirect(offsets[:]), dx[t][:])
-            (nc.scalar if t == LANES - 1 else nc.sync).dma_start(out_rows[:, t, :], window[t][:])
-            for c in range(len(OUT_CHUNKS)):
-                round_plane(t, c)
+        g_round(0)
+        quantize_wv(0)
+        g_quantize(0)
+        early = ps.tile([P, HALF], F32, name="score0")
+        back(early[:], 1, halves[0])
+        dx1 = [tile("dx1%d" % h, [P, HALF], F32) for h in range(2)]
+        nc.scalar.copy(dx1[0][:], early[:])
+        nc.scalar.activation(listed(1, 0), dx1[0][:], ACT.Copy)
+        g_round(1)
+        quantize_wv(1)
+        g_quantize(1)
+
+        late = ps.tile([P, HALF], F32, name="grad1")
+        back(late[:], 1, halves[1])
+        grad = {t: ps.tile([P, N], F32, name="grad%d" % t) for t in (0, 3, 2)}
+        for t in (0, 3, 2):
+            back(grad[t][:], t, slice(0, N))
+        dx = {t: tile("dx%d" % t, [P, N], F32) for t in (0, 3, 2)}
+
+        nc.scalar.copy(dx1[1][:], late[:])
+        nc.scalar.activation(listed(1, 1), dx1[1][:], ACT.Copy)
+        store_plane(1)
+        nc.vector.tensor_copy(dx[0][:], grad[0][:])
+        nc.vector.tensor_copy(window[0][:].indirect(offsets[:]), dx[0][:])
+        store_plane(0)
+        nc.scalar.copy(dx[3][:], grad[3][:])
+        for h in range(2):
+            nc.scalar.activation(listed(3, h), dx[3][:, halves[h]], ACT.Copy)
+        store_plane(3)
+        nc.vector.tensor_copy(dx[2][:], grad[2][:])
+        nc.vector.tensor_copy(window[2][:].indirect(offsets[:]), dx[2][:])
+        store_plane(2)
+
+        last = len(OUT_CHUNKS) - 1
+        for t in (1, 0):
+            for c in range(last):
+                round_plane("gpsimd", t, c)
+        for t in (1, 0):
+            round_plane("scalar", t, last)
 
         out_words = out_1.rearrange("o p t l -> p (o t l)").bitcast(I32)
         out_s = tile("out_s", [P, T], U8)
@@ -234,15 +229,23 @@ def tile_attend_gml_pl_sqh_kernel(tc, xT, wd, wv, y, cw, rw, offs, out_0, out_1,
             nc.vector.quantize_mx(out=out_q[c][:].bitcast(E4M3), scales=out_s[:, cols], in_=quads[c][:].rearrange("p n l -> p (n l)"))
             nc.sync.dma_start(out_words[:, cols], out_q[c][:].bitcast(I32))
 
+        for c in (3, 4):
+            for t in (3, 2):
+                round_plane("scalar", t, c)
+            weave(c, nc.scalar.copy, U32)
+        for c in (0, 1):
+            for t in (3, 2):
+                round_plane("vector", t, c)
         weave(0, nc.vector.tensor_copy, I32)
         weave(1, nc.vector.tensor_copy, I32)
         out_quantize(0)
-        weave(2, nc.vector.tensor_copy, I32)
+        for t in (3, 2):
+            round_plane("vector", t, 2)
         out_quantize(1)
-        weave(3, nc.scalar.copy, U32)
-        weave(4, nc.scalar.copy, U32)
-        for c in range(2, len(OUT_CHUNKS)):
-            out_quantize(c)
+        weave(2, nc.vector.tensor_copy, I32)
+        out_quantize(3)
+        out_quantize(2)
+        out_quantize(4)
         for q in range(4):
             queue = nc.scalar if q % 2 else nc.sync
             queue.dma_start(out_2[0, 4 * q : 4 * q + 4, :].bitcast(I32), out_s[32 * q : 32 * q + 4, :].bitcast(I32))

@@ -19,19 +19,24 @@ ACT = mybir.ActivationFunctionType
 
 P = 128
 LANES = 4
-G_CHUNK = 256
-OUT_CHUNKS = (512, 512, 256, 256, 512)
+OUT_CHUNKS = (512, 512, 512, 256, 256)
+VECTOR_CHUNKS = 2
 HALF = N // 2
+PAIR = 2 * P * LANES
 
 
 def tile_attend_gml_pl_sqh_kernel(tc, xT, wd, wv, y, cw, rw, offs, out_0, out_1, out_2):
     nc = tc.nc
     with ExitStack() as ctx:
         sb = ctx.enter_context(tc.tile_pool(name="sb", bufs=1))
+        shared = ctx.enter_context(tc.tile_pool(name="shared", bufs=1))
         ps = ctx.enter_context(tc.psum_pool(name="ps", bufs=1))
 
         def tile(name, shape, dtype, tag=None):
             return sb.tile(shape, dtype, name=name, tag=tag or name, align_bytes=64)
+
+        def placed(name, shape, dtype, kib):
+            return shared.tile(shape, dtype, name=name, align_bytes=64, offset=1024 * kib)
 
         x_rows = xT.rearrange("(p j) t -> p j t", j=LANES)
         wd_rows = wd.rearrange("(p j) v -> p j v", j=LANES)
@@ -50,11 +55,9 @@ def tile_attend_gml_pl_sqh_kernel(tc, xT, wd, wv, y, cw, rw, offs, out_0, out_1,
             nc.sync.dma_start(x_plane[j][:], x_rows[:, j, :])
         wd_raw = tile("wd_raw", [P, LANES, V], F32)
         nc.sync.dma_start(wd_raw[:], wd_rows)
-        y_all = tile("y_all", [P, 6, N], F32)
-        y_pair = [y_all[:, 4 * h : 4 * h + 2, :] for h in range(2)]
+        y_all = tile("y_all", [P, LANES, N], F32)
         for h in range(2):
-            nc.sync.dma_start(y_pair[h], y_rows[:, 2 * h : 2 * h + 2, :])
-        y_sb = [y_pair[r // 2][:, r % 2, :] for r in range(LANES)]
+            nc.sync.dma_start(y_all[:, 2 * h : 2 * h + 2, :], y_rows[:, 2 * h : 2 * h + 2, :])
         wv_raw = tile("wv_raw", [P, LANES, D], F32)
         nc.sync.dma_start(wv_raw[:], wv_rows)
 
@@ -82,71 +85,76 @@ def tile_attend_gml_pl_sqh_kernel(tc, xT, wd, wv, y, cw, rw, offs, out_0, out_1,
         x_s = tile("x_s", [P, N], U8)
         nc.vector.quantize_mx(out=x_q[:].bitcast(E4M3), scales=x_s[:], in_=x_b[:].rearrange("p n j -> p (n j)"))
 
-        def deal(copy, dealt, raw, s_range, r_range):
+        def deal(copy, dealt, raw, h):
             copy(
-                dealt[:, r_range, s_range, :].rearrange("p r s j -> p s j r"),
-                raw[:].rearrange("p j (s r) -> p s j r", r=LANES)[:, s_range, :, r_range],
+                dealt.rearrange("p (r s j) -> p s j r", r=2, j=LANES),
+                raw[:].rearrange("p j (s r) -> p s j r", r=LANES)[:, :, :, 2 * h : 2 * h + 2],
             )
 
-        def quantize_head(dealt, codes, scales, r):
+        def quantize_pair(dealt, codes, scales, h):
+            rows = slice(2 * h, 2 * h + 2)
             nc.vector.quantize_mx(
-                out=codes[:, r, :].bitcast(E4M3), scales=scales[:, r, :], in_=dealt[:, r, :, :].rearrange("p s j -> p (s j)")
+                out=codes[:, rows, :].rearrange("p r s -> p (r s)").bitcast(E4M3), scales=scales[:, rows, :].rearrange("p r s -> p (r s)"), in_=dealt
             )
 
-        wd_b = tile("wd_b", [P, LANES, P, LANES], BF16)
-        deal(nc.vector.tensor_copy, wd_b, wd_raw, slice(0, P), slice(0, 2))
-        deal(nc.scalar.copy, wd_b, wd_raw, slice(0, P), slice(2, LANES))
+        wd_b = [tile("wd_b0", [P, PAIR], BF16)[:], placed("wd_b1", [P, 4 * PAIR], BF16, 0)[:, :PAIR]]
+        deal(nc.vector.tensor_copy, wd_b[0], wd_raw, 0)
+        deal(nc.scalar.copy, wd_b[1], wd_raw, 1)
         wd_q = tile("wd_q", [P, LANES, P], U32)
         wd_s = tile("wd_s", [P, LANES, P], U8)
-        score = [ps.tile([P, N], F32, name="score%d" % r) for r in range(LANES)]
-        for r in range(LANES):
-            quantize_head(wd_b, wd_q, wd_s, r)
-            nc.tensor.matmul_mx(
-                out=score[r][:], lhsT=wd_q[:, r, :].bitcast(E4M3), lhsT_scale=wd_s[:, r, :],
-                rhs=x_q[:].bitcast(E4M3), rhs_scale=x_s[:], start=True, stop=True,
-            )
+        halves = [slice(h * HALF, (h + 1) * HALF) for h in range(2)]
+        row_pairs = [slice(2 * k, 2 * k + 2) for k in range(2)]
+        score = {(h, k): ps.tile([P, 2, HALF], F32, name="score%d" % (2 * h + k)) for h in range(2) for k in range(2)}
+        for k in range(2):
+            quantize_pair(wd_b[k], wd_q, wd_s, k)
+        for h in range(2):
+            for r in range(LANES):
+                nc.tensor.matmul_mx(
+                    out=score[h, r // 2][:, r % 2, :], lhsT=wd_q[:, r, :].bitcast(E4M3), lhsT_scale=wd_s[:, r, :],
+                    rhs=x_q[:, halves[h]].bitcast(E4M3), rhs_scale=x_s[:, halves[h]], start=True, stop=True,
+                )
 
-        margin = [tile("margin%d" % r, [P, N], F32) for r in range(LANES)]
+        work = placed("work", [P, LANES * N], F32, 6)
+        rows = work[:].rearrange("p (r i) -> p r i", r=LANES)
+        margin = {
+            (0, 0): placed("margin00", [P, N], F32, 4)[:], (0, 1): rows[:, 2, :],
+            (1, 0): rows[:, 3, :], (1, 1): tile("margin11", [P, N], F32)[:],
+        }
+        coef = [placed("coef0", [P, LANES, HALF], F32, 0)[:], rows[:, :, :HALF]]
+        wv_b = [rows[:, 3, :].bitcast(BF16), placed("wv_b1", [P, PAIR], BF16, 0)[:]]
+        g_b = [rows[:, 2, :].bitcast(BF16), tile("g_b1", [P, HALF * LANES], BF16)[:]]
         hinge = tile("hinge", [P, LANES, N], F32)
-        coef = [tile("coef0", [P, LANES, G_CHUNK], F32, tag="wd_b")[:], y_all[:, 2:, G_CHUNK:]]
-        nc.vector.tensor_tensor(coef[1][:, :2, :], y_pair[0][:, :, G_CHUNK:], weight[:, :2, G_CHUNK:], ALU.mult)
-        for h in range(2):
-            nc.gpsimd.tensor_tensor(coef[0][:, 2 * h : 2 * h + 2, :], y_pair[h][:, :, :G_CHUNK], weight[:, 2 * h : 2 * h + 2, :G_CHUNK], ALU.mult)
-        for r in range(LANES):
-            nc.vector.tensor_tensor(margin[r][:], y_sb[r], score[r][:], ALU.mult)
-            nc.scalar.activation(hinge[:, r, :], margin[r][:], ACT.Relu, bias=1.0, scale=-1.0)
-        nc.vector.tensor_tensor(coef[1][:, 2:, :], y_pair[1][:, :, G_CHUNK:], weight[:, 2:, G_CHUNK:], ALU.mult)
 
-        wv_b = tile("wv_b", [P, LANES, P, LANES], BF16)
+        def coefficients(engine, h, k):
+            engine.tensor_tensor(coef[h][:, row_pairs[k], :], y_all[:, row_pairs[k], halves[h]], weight[:, row_pairs[k], halves[h]], ALU.mult)
+
+        coefficients(nc.vector, 1, 0)
+        for k in range(2):
+            coefficients(nc.gpsimd, 0, k)
         for h in range(2):
-            deal(nc.scalar.copy, wv_b, wv_raw, slice(0, P), slice(2 * h, 2 * h + 2))
+            for k in range(2):
+                m = margin[h, k].rearrange("p (r i) -> p r i", r=2)
+                nc.vector.tensor_tensor(m, y_all[:, row_pairs[k], halves[h]], score[h, k][:], ALU.mult)
+                if (h, k) == (1, 1):
+                    deal(nc.scalar.copy, wv_b[0], wv_raw, 0)
+                nc.scalar.activation(hinge[:, row_pairs[k], halves[h]], m, ACT.Relu, bias=1.0, scale=-1.0)
 
         g_q = tile("g_q", [P, N], U32)
         g_s = tile("g_s", [P, N], U8)
-        g_b = [tile("g_b%d" % h, [P, HALF, LANES], BF16) for h in range(2)]
-        halves = [slice(h * HALF, (h + 1) * HALF) for h in range(2)]
 
         def g_round(h):
             nc.vector.tensor_tensor(
-                g_b[h][:].rearrange("p (c i) r -> p c r i", i=4),
+                g_b[h].rearrange("p (c i r) -> p c r i", i=4, r=LANES),
                 hinge[:, :, halves[h]].rearrange("p r (c i) -> p c r i", i=4),
                 coef[h].rearrange("p r (c i) -> p c r i", i=4),
                 ALU.mult,
             )
 
         def g_quantize(h):
-            nc.vector.quantize_mx(out=g_q[:, halves[h]].bitcast(E5M2), scales=g_s[:, halves[h]], in_=g_b[h][:].rearrange("p n r -> p (n r)"))
+            nc.vector.quantize_mx(out=g_q[:, halves[h]].bitcast(E5M2), scales=g_s[:, halves[h]], in_=g_b[h])
 
         wv_q = tile("wv_q", [P, LANES, P], U32)
         wv_s = tile("wv_s", [P, LANES, P], U8)
-
-        def quantize_wv(h):
-            rows = slice(2 * h, 2 * h + 2)
-            nc.vector.quantize_mx(
-                out=wv_q[:, rows, :].rearrange("p r s -> p (r s)").bitcast(E4M3),
-                scales=wv_s[:, rows, :].rearrange("p r s -> p (r s)"),
-                in_=wv_b[:, rows, :, :].rearrange("p r s j -> p (r s j)"),
-            )
 
         def back(bank, t, cols):
             nc.tensor.matmul_mx(
@@ -158,60 +166,58 @@ def tile_attend_gml_pl_sqh_kernel(tc, xT, wd, wv, y, cw, rw, offs, out_0, out_1,
             return window[t][:].indirect(offsets[:, h * HALF // 16 : (h + 1) * HALF // 16])
 
         def store_plane(t):
-            (nc.scalar if t == 2 else nc.sync).dma_start(out_rows[:, t, :], window[t][:])
+            (nc.scalar if t == LANES - 1 else nc.sync).dma_start(out_rows[:, t, :], window[t][:])
 
         starts = [sum(OUT_CHUNKS[:c]) for c in range(len(OUT_CHUNKS))]
         pairs = [tile("pairs%d" % c, [P, 2, n, 2], BF16) for c, n in enumerate(OUT_CHUNKS)]
 
-        def round_plane(engine, t, c):
-            src = window[t][:, starts[c] : starts[c] + OUT_CHUNKS[c]]
-            dst = pairs[c][:, t // 2, :, t % 2]
-            if engine == "gpsimd":
-                nc.gpsimd.tensor_scalar(dst, src, 1.0, -0.0, ALU.mult, ALU.add)
-            elif engine == "vector":
-                nc.vector.tensor_copy(dst, src)
+        def round_plane(t, c):
+            n = OUT_CHUNKS[c]
+            src = window[t][:, starts[c] : starts[c] + n]
+            if c < VECTOR_CHUNKS or t < 2:
+                nc.vector.tensor_copy(pairs[c][:, t // 2, :, t % 2], src)
+            elif t == 2:
+                nc.vector.tensor_copy(pairs[c][:, 1, :, :], src.unsqueeze(2).to_broadcast([P, n, 2]))
             else:
-                nc.scalar.copy(dst, src)
+                nc.scalar.copy(pairs[c][:, 1, :, 1], src)
+
+        dx = {(t, h): tile("dx%d%d" % (t, h), [P, HALF], F32)[:] for t in range(2) for h in range(2)}
+
+        def bring(t, cols, bank_name, copy, dst):
+            bank = ps.tile([P, cols.stop - cols.start], F32, name=bank_name)
+            back(bank[:], t, cols)
+            copy(dst, bank[:])
+
+        def scatter(t, h):
+            if (t, h) == (LANES - 1, 0):
+                nc.vector.tensor_copy(listed(t, h), dx[t, h])
+            else:
+                nc.scalar.activation(listed(t, h), dx[t, h], ACT.Copy)
 
         g_round(0)
-        quantize_wv(0)
+        quantize_pair(wv_b[0], wv_q, wv_s, 0)
         g_quantize(0)
-        early = ps.tile([P, HALF], F32, name="score0")
-        back(early[:], 1, halves[0])
-        dx1 = [tile("dx1%d" % h, [P, HALF], F32) for h in range(2)]
-        nc.scalar.copy(dx1[0][:], early[:])
-        nc.scalar.activation(listed(1, 0), dx1[0][:], ACT.Copy)
+        bring(0, halves[0], "score0", nc.scalar.copy, dx[0, 0])
+        deal(nc.vector.tensor_copy, wv_b[1], wv_raw, 1)
+        bring(1, halves[0], "score1", nc.vector.tensor_copy, dx[1, 0])
+        coefficients(nc.vector, 1, 1)
+        quantize_pair(wv_b[1], wv_q, wv_s, 1)
         g_round(1)
-        quantize_wv(1)
         g_quantize(1)
-
-        late = ps.tile([P, HALF], F32, name="grad1")
-        back(late[:], 1, halves[1])
-        grad = {t: ps.tile([P, N], F32, name="grad%d" % t) for t in (0, 3, 2)}
-        for t in (0, 3, 2):
-            back(grad[t][:], t, slice(0, N))
-        dx = {t: tile("dx%d" % t, [P, N], F32) for t in (0, 3, 2)}
-
-        nc.scalar.copy(dx1[1][:], late[:])
-        nc.scalar.activation(listed(1, 1), dx1[1][:], ACT.Copy)
-        store_plane(1)
-        nc.vector.tensor_copy(dx[0][:], grad[0][:])
-        nc.vector.tensor_copy(window[0][:].indirect(offsets[:]), dx[0][:])
-        store_plane(0)
-        nc.scalar.copy(dx[3][:], grad[3][:])
-        for h in range(2):
-            nc.scalar.activation(listed(3, h), dx[3][:, halves[h]], ACT.Copy)
-        store_plane(3)
-        nc.vector.tensor_copy(dx[2][:], grad[2][:])
-        nc.vector.tensor_copy(window[2][:].indirect(offsets[:]), dx[2][:])
-        store_plane(2)
-
-        last = len(OUT_CHUNKS) - 1
-        for t in (1, 0):
-            for c in range(last):
-                round_plane("gpsimd", t, c)
-        for t in (1, 0):
-            round_plane("scalar", t, last)
+        for t in range(2):
+            bring(t, halves[1], "grad%d" % t, nc.vector.tensor_copy, dx[t, 1])
+        for t in range(2, LANES):
+            whole = tile("dx%d" % t, [P, N], F32)
+            bring(t, slice(0, N), "grad%d" % t, nc.vector.tensor_copy, whole[:])
+            for h in range(2):
+                dx[t, h] = whole[:, halves[h]]
+        for t, h in ((0, 0), (1, 0), (0, 1), (1, 1), (3, 0), (2, 0), (2, 1), (3, 1)):
+            scatter(t, h)
+        for t in range(LANES):
+            store_plane(t)
+            if t < LANES - 1:
+                for c in range(len(OUT_CHUNKS)):
+                    round_plane(t, c)
 
         out_words = out_1.rearrange("o p t l -> p (o t l)").bitcast(I32)
         out_s = tile("out_s", [P, T], U8)
@@ -229,23 +235,15 @@ def tile_attend_gml_pl_sqh_kernel(tc, xT, wd, wv, y, cw, rw, offs, out_0, out_1,
             nc.vector.quantize_mx(out=out_q[c][:].bitcast(E4M3), scales=out_s[:, cols], in_=quads[c][:].rearrange("p n l -> p (n l)"))
             nc.sync.dma_start(out_words[:, cols], out_q[c][:].bitcast(I32))
 
-        for c in (3, 4):
-            for t in (3, 2):
-                round_plane("scalar", t, c)
+        for c in range(VECTOR_CHUNKS, len(OUT_CHUNKS)):
+            round_plane(LANES - 1, c)
             weave(c, nc.scalar.copy, U32)
-        for c in (0, 1):
-            for t in (3, 2):
-                round_plane("vector", t, c)
-        weave(0, nc.vector.tensor_copy, I32)
-        weave(1, nc.vector.tensor_copy, I32)
-        out_quantize(0)
-        for t in (3, 2):
-            round_plane("vector", t, 2)
-        out_quantize(1)
-        weave(2, nc.vector.tensor_copy, I32)
-        out_quantize(3)
-        out_quantize(2)
-        out_quantize(4)
+        for c in range(VECTOR_CHUNKS):
+            round_plane(LANES - 1, c)
+        for c in range(VECTOR_CHUNKS):
+            weave(c, nc.vector.tensor_copy, I32)
+        for c in range(len(OUT_CHUNKS)):
+            out_quantize(c)
         for q in range(4):
             queue = nc.scalar if q % 2 else nc.sync
             queue.dma_start(out_2[0, 4 * q : 4 * q + 4, :].bitcast(I32), out_s[32 * q : 32 * q + 4, :].bitcast(I32))

@@ -21,6 +21,9 @@ P = 128
 LANES = 4
 OUT_CHUNKS = (512, 512, 512, 256, 256)
 VECTOR_CHUNKS = 2
+SPAN = 512
+GPSIMD_COLUMNS = 512
+LAST = LANES - 1
 HALF = N // 2
 PAIR = 2 * P * LANES
 
@@ -46,7 +49,7 @@ def tile_attend_gml_pl_sqh_kernel(tc, xT, wd, wv, y, cw, rw, offs, out_0, out_1,
 
         offsets = sb.tile([P, N // 16], U16, name="offsets")
         nc.sync.dma_start(offsets[:], offs)
-        cw_sb = tile("cw_sb", [P, LANES], F32)
+        cw_sb = tile("cw_sb", [P, LANES], F32, tag="window2")
         nc.scalar.dma_start(cw_sb[:], cw.rearrange("(p j) o -> p (j o)", j=LANES))
         rw_sb = tile("rw_sb", [P, LANES], F32)
         nc.scalar.dma_start(rw_sb[:], rw[0:1, :].rearrange("o (p c) -> p (o c)", c=LANES))
@@ -61,16 +64,19 @@ def tile_attend_gml_pl_sqh_kernel(tc, xT, wd, wv, y, cw, rw, offs, out_0, out_1,
         wv_raw = tile("wv_raw", [P, LANES, D], F32)
         nc.sync.dma_start(wv_raw[:], wv_rows)
 
-        window = [tile("window%d" % t, [P, T], F32) for t in range(LANES)]
-        for t in range(LANES):
+        window = {t: tile("window%d" % t, [P, T], F32) for t in range(2)}
+        for t in range(2):
             nc.vector.memset(window[t][:], 0.0)
 
         ident = tile("ident", [P, P], F32)
         make_identity(nc, ident[:])
-        minus_one = tile("minus_one", [P, LANES], F32)
+        minus_one = tile("minus_one", [P, LANES], F32, tag="window3")
         nc.gpsimd.memset(minus_one[:], -1.0)
         neg_cw = tile("neg_cw", [P, LANES], F32)
         nc.gpsimd.tensor_tensor(neg_cw[:], cw_sb[:], minus_one[:], ALU.mult)
+        for t in range(2, LANES):
+            window[t] = tile("window%d" % t, [P, T], F32)
+            nc.gpsimd.memset(window[t][:], 0.0)
         rw_all = ps.tile([P, LANES, P], F32, name="grad3")
         for c in range(LANES):
             nc.tensor.transpose(rw_all[:, c, :], rw_sb[:, c : c + 1].to_broadcast([P, P]), ident[:])
@@ -79,11 +85,18 @@ def tile_attend_gml_pl_sqh_kernel(tc, xT, wd, wv, y, cw, rw, offs, out_0, out_1,
             nc.scalar.mul(weight[:, r, :].rearrange("m (p c) -> m p c", c=LANES), rw_all[:].rearrange("m c p -> m p c"), neg_cw[:, r : r + 1])
 
         x_b = tile("x_b", [P, N, LANES], BF16)
-        for j in range(LANES):
+        halves = [slice(h * HALF, (h + 1) * HALF) for h in range(2)]
+        half_list = [offsets[:, h * HALF // 16 : (h + 1) * HALF // 16] for h in range(2)]
+        for j in range(LANES - 1):
             nc.vector.tensor_copy(x_b[:, :, j], x_plane[j][:].indirect(offsets[:]))
+        for h in range(2):
+            nc.vector.tensor_copy(x_b[:, halves[h], LANES - 1], x_plane[LANES - 1][:].indirect(half_list[h]))
         x_q = tile("x_q", [P, N], U32)
         x_s = tile("x_s", [P, N], U8)
-        nc.vector.quantize_mx(out=x_q[:].bitcast(E4M3), scales=x_s[:], in_=x_b[:].rearrange("p n j -> p (n j)"))
+        for h in range(2):
+            nc.vector.quantize_mx(
+                out=x_q[:, halves[h]].bitcast(E4M3), scales=x_s[:, halves[h]], in_=x_b[:, halves[h], :].rearrange("p n j -> p (n j)")
+            )
 
         def deal(copy, dealt, raw, h):
             copy(
@@ -102,7 +115,6 @@ def tile_attend_gml_pl_sqh_kernel(tc, xT, wd, wv, y, cw, rw, offs, out_0, out_1,
         deal(nc.scalar.copy, wd_b[1], wd_raw, 1)
         wd_q = tile("wd_q", [P, LANES, P], U32)
         wd_s = tile("wd_s", [P, LANES, P], U8)
-        halves = [slice(h * HALF, (h + 1) * HALF) for h in range(2)]
         row_pairs = [slice(2 * k, 2 * k + 2) for k in range(2)]
         score = {(h, k): ps.tile([P, 2, HALF], F32, name="score%d" % (2 * h + k)) for h in range(2) for k in range(2)}
         for k in range(2):
@@ -117,12 +129,12 @@ def tile_attend_gml_pl_sqh_kernel(tc, xT, wd, wv, y, cw, rw, offs, out_0, out_1,
         work = placed("work", [P, LANES * N], F32, 6)
         rows = work[:].rearrange("p (r i) -> p r i", r=LANES)
         margin = {
-            (0, 0): placed("margin00", [P, N], F32, 4)[:], (0, 1): rows[:, 2, :],
-            (1, 0): rows[:, 3, :], (1, 1): tile("margin11", [P, N], F32)[:],
+            (0, 0): rows[:, 2, :], (0, 1): rows[:, 3, :],
+            (1, 0): placed("margin10", [P, N], F32, 4)[:], (1, 1): tile("margin11", [P, N], F32)[:],
         }
         coef = [placed("coef0", [P, LANES, HALF], F32, 0)[:], rows[:, :, :HALF]]
-        wv_b = [rows[:, 3, :].bitcast(BF16), placed("wv_b1", [P, PAIR], BF16, 0)[:]]
-        g_b = [rows[:, 2, :].bitcast(BF16), tile("g_b1", [P, HALF * LANES], BF16)[:]]
+        wv_b = [rows[:, 3, :].bitcast(BF16), placed("wv_b1", [P, PAIR], BF16, 14)[:]]
+        g_b = [rows[:, 2, :].bitcast(BF16), placed("g_b1", [P, HALF * LANES], BF16, 14)[:]]
         hinge = tile("hinge", [P, LANES, N], F32)
 
         def coefficients(engine, h, k):
@@ -135,7 +147,7 @@ def tile_attend_gml_pl_sqh_kernel(tc, xT, wd, wv, y, cw, rw, offs, out_0, out_1,
             for k in range(2):
                 m = margin[h, k].rearrange("p (r i) -> p r i", r=2)
                 nc.vector.tensor_tensor(m, y_all[:, row_pairs[k], halves[h]], score[h, k][:], ALU.mult)
-                if (h, k) == (1, 1):
+                if (h, k) == (1, 0):
                     deal(nc.scalar.copy, wv_b[0], wv_raw, 0)
                 nc.scalar.activation(hinge[:, row_pairs[k], halves[h]], m, ACT.Relu, bias=1.0, scale=-1.0)
 
@@ -163,61 +175,74 @@ def tile_attend_gml_pl_sqh_kernel(tc, xT, wd, wv, y, cw, rw, offs, out_0, out_1,
             )
 
         def listed(t, h):
-            return window[t][:].indirect(offsets[:, h * HALF // 16 : (h + 1) * HALF // 16])
+            return window[t][:].indirect(half_list[h])
 
         def store_plane(t):
-            (nc.scalar if t == LANES - 1 else nc.sync).dma_start(out_rows[:, t, :], window[t][:])
+            (nc.scalar if t == LAST else nc.sync).dma_start(out_rows[:, t, :], window[t][:])
 
         starts = [sum(OUT_CHUNKS[:c]) for c in range(len(OUT_CHUNKS))]
-        pairs = [tile("pairs%d" % c, [P, 2, n, 2], BF16) for c, n in enumerate(OUT_CHUNKS)]
+        spans = [(first, SPAN) for first in range(0, T, SPAN)]
+        pair_tiles = [tile("pairs%d" % k, [P, 2, n, 2], BF16) for k, (first, n) in enumerate(spans)]
 
-        def round_plane(t, c):
-            n = OUT_CHUNKS[c]
-            src = window[t][:, starts[c] : starts[c] + n]
-            if c < VECTOR_CHUNKS or t < 2:
-                nc.vector.tensor_copy(pairs[c][:, t // 2, :, t % 2], src)
-            elif t == 2:
-                nc.vector.tensor_copy(pairs[c][:, 1, :, :], src.unsqueeze(2).to_broadcast([P, n, 2]))
+        def pairs(c):
+            k, at = divmod(starts[c], SPAN)
+            return pair_tiles[k][:, :, at : at + OUT_CHUNKS[c], :]
+
+        def round_early(t, k):
+            first, n = spans[k]
+            src = window[t][:, first : first + n]
+            done = min(max(GPSIMD_COLUMNS - first, 0), n) if t == 0 else 0
+            if done:
+                both = src[:, :done].unsqueeze(2).to_broadcast([P, done, 2])
+                nc.gpsimd.tensor_scalar(pair_tiles[k][:, 0, :done, :], both, 1.0, -0.0, ALU.mult, ALU.add)
+            if done == n:
+                return
+            if k < VECTOR_CHUNKS or t < 2:
+                nc.vector.tensor_copy(pair_tiles[k][:, t // 2, done:, t % 2], src[:, done:])
             else:
-                nc.scalar.copy(pairs[c][:, 1, :, 1], src)
+                nc.vector.tensor_copy(pair_tiles[k][:, 1, :, :], src.unsqueeze(2).to_broadcast([P, n, 2]))
 
-        dx = {(t, h): tile("dx%d%d" % (t, h), [P, HALF], F32)[:] for t in range(2) for h in range(2)}
+        def round_last(k, copy):
+            copy(pair_tiles[k][:, 1, :, 1], window[LAST][:, k * SPAN : (k + 1) * SPAN])
 
-        def bring(t, cols, bank_name, copy, dst):
-            bank = ps.tile([P, cols.stop - cols.start], F32, name=bank_name)
+        def bring(t, cols, bank_name, copy):
+            n = cols.stop - cols.start
+            bank = ps.tile([P, n], F32, name=bank_name)
             back(bank[:], t, cols)
-            copy(dst, bank[:])
+            dx = tile("dx%d_%d" % (t, cols.start), [P, n], F32)[:]
+            copy(dx, bank[:])
+            return dx
 
         def scatter(t, h):
-            if (t, h) == (LANES - 1, 0):
+            if (t, h) == (3, 0):
                 nc.vector.tensor_copy(listed(t, h), dx[t, h])
             else:
                 nc.scalar.activation(listed(t, h), dx[t, h], ACT.Copy)
 
+        dx = {}
         g_round(0)
         quantize_pair(wv_b[0], wv_q, wv_s, 0)
         g_quantize(0)
-        bring(0, halves[0], "score0", nc.scalar.copy, dx[0, 0])
-        deal(nc.vector.tensor_copy, wv_b[1], wv_raw, 1)
-        bring(1, halves[0], "score1", nc.vector.tensor_copy, dx[1, 0])
+        dx[0, 0] = bring(0, halves[0], "score0", nc.scalar.copy)
         coefficients(nc.vector, 1, 1)
-        quantize_pair(wv_b[1], wv_q, wv_s, 1)
+        dx[1, 0] = bring(1, halves[0], "score1", nc.vector.tensor_copy)
         g_round(1)
         g_quantize(1)
-        for t in range(2):
-            bring(t, halves[1], "grad%d" % t, nc.vector.tensor_copy, dx[t, 1])
+        deal(nc.vector.tensor_copy, wv_b[1], wv_raw, 1)
+        dx[0, 1] = bring(0, halves[1], "grad0", nc.vector.tensor_copy)
+        quantize_pair(wv_b[1], wv_q, wv_s, 1)
+        dx[1, 1] = bring(1, halves[1], "grad1", nc.vector.tensor_copy)
         for t in range(2, LANES):
-            whole = tile("dx%d" % t, [P, N], F32)
-            bring(t, slice(0, N), "grad%d" % t, nc.vector.tensor_copy, whole[:])
+            whole = bring(t, slice(0, N), "grad%d" % t, nc.vector.tensor_copy)
             for h in range(2):
                 dx[t, h] = whole[:, halves[h]]
         for t, h in ((0, 0), (1, 0), (0, 1), (1, 1), (3, 0), (2, 0), (2, 1), (3, 1)):
             scatter(t, h)
         for t in range(LANES):
             store_plane(t)
-            if t < LANES - 1:
-                for c in range(len(OUT_CHUNKS)):
-                    round_plane(t, c)
+            if t != LAST:
+                for k in range(len(spans)):
+                    round_early(t, k)
 
         out_words = out_1.rearrange("o p t l -> p (o t l)").bitcast(I32)
         out_s = tile("out_s", [P, T], U8)
@@ -227,7 +252,7 @@ def tile_attend_gml_pl_sqh_kernel(tc, xT, wd, wv, y, cw, rw, offs, out_0, out_1,
         def weave(c, copy, word):
             copy(
                 quads[c][:].rearrange("p n l -> p (n l)").bitcast(word).rearrange("p (c i u) -> p c u i", i=2, u=2),
-                pairs[c][:].rearrange("p u n e -> p (u n e)").bitcast(word).rearrange("p (u c i) -> p c u i", u=2, i=2),
+                pairs(c).rearrange("p u n e -> p u (n e)").bitcast(word).rearrange("p u (c i) -> p c u i", i=2),
             )
 
         def out_quantize(c):
@@ -235,11 +260,12 @@ def tile_attend_gml_pl_sqh_kernel(tc, xT, wd, wv, y, cw, rw, offs, out_0, out_1,
             nc.vector.quantize_mx(out=out_q[c][:].bitcast(E4M3), scales=out_s[:, cols], in_=quads[c][:].rearrange("p n l -> p (n l)"))
             nc.sync.dma_start(out_words[:, cols], out_q[c][:].bitcast(I32))
 
+        for k in range(VECTOR_CHUNKS, len(spans)):
+            round_last(k, nc.scalar.copy)
         for c in range(VECTOR_CHUNKS, len(OUT_CHUNKS)):
-            round_plane(LANES - 1, c)
             weave(c, nc.scalar.copy, U32)
         for c in range(VECTOR_CHUNKS):
-            round_plane(LANES - 1, c)
+            round_last(c, nc.vector.tensor_copy)
         for c in range(VECTOR_CHUNKS):
             weave(c, nc.vector.tensor_copy, I32)
         for c in range(len(OUT_CHUNKS)):

@@ -182,7 +182,7 @@ def tile_attend_gml_pl_sqh_kernel(tc, xT, wd, wv, y, cw, rw, offs, out_0, out_1,
 
         starts = [sum(OUT_CHUNKS[:c]) for c in range(len(OUT_CHUNKS))]
         spans = [(first, SPAN) for first in range(0, T, SPAN)]
-        pair_tiles = [tile("pairs%d" % k, [P, 2, n, 2], BF16) for k, (first, n) in enumerate(spans)]
+        pair_tiles = [tile("pairs0", [P, 2, SPAN, 2], BF16)] + [placed("pairs%d" % k, [P, 2, SPAN, 2], BF16, 12 + 4 * k) for k in range(1, len(spans))]
 
         def pairs(c):
             k, at = divmod(starts[c], SPAN)
@@ -205,16 +205,17 @@ def tile_attend_gml_pl_sqh_kernel(tc, xT, wd, wv, y, cw, rw, offs, out_0, out_1,
         def round_last(k, copy):
             copy(pair_tiles[k][:, 1, :, 1], window[LAST][:, k * SPAN : (k + 1) * SPAN])
 
-        def bring(t, cols, bank_name, copy):
+        def bring(t, cols, bank_name, copy, dx=None):
             n = cols.stop - cols.start
             bank = ps.tile([P, n], F32, name=bank_name)
             back(bank[:], t, cols)
-            dx = tile("dx%d_%d" % (t, cols.start), [P, n], F32)[:]
+            if dx is None:
+                dx = tile("dx%d_%d" % (t, cols.start), [P, n], F32)[:]
             copy(dx, bank[:])
             return dx
 
         def scatter(t, h):
-            if (t, h) == (3, 0):
+            if (t, h) == (2, 1):
                 nc.vector.tensor_copy(listed(t, h), dx[t, h])
             else:
                 nc.scalar.activation(listed(t, h), dx[t, h], ACT.Copy)
@@ -232,11 +233,20 @@ def tile_attend_gml_pl_sqh_kernel(tc, xT, wd, wv, y, cw, rw, offs, out_0, out_1,
         dx[0, 1] = bring(0, halves[1], "grad0", nc.vector.tensor_copy)
         quantize_pair(wv_b[1], wv_q, wv_s, 1)
         dx[1, 1] = bring(1, halves[1], "grad1", nc.vector.tensor_copy)
-        for t in range(2, LANES):
-            whole = bring(t, slice(0, N), "grad%d" % t, nc.vector.tensor_copy)
-            for h in range(2):
-                dx[t, h] = whole[:, halves[h]]
-        for t, h in ((0, 0), (1, 0), (0, 1), (1, 1), (3, 0), (2, 0), (2, 1), (3, 1)):
+        for h in range(2):
+            for t in range(2):
+                scatter(t, h)
+        bank = ps.tile([P, N], F32, name="grad2")
+        back(bank[:], 2, slice(0, N))
+        dx[2, 1] = placed("dx2_vector", [P, 10 * HALF], F32, 19)[:, :HALF]
+        dx[2, 0] = tile("dx2_scalar", [P, HALF], F32)[:]
+        for h in (1, 0):
+            nc.vector.tensor_copy(dx[2, h], bank[:, halves[h]])
+        scatter(2, 1)
+        whole = bring(3, slice(0, N), "grad3", nc.vector.tensor_copy, placed("dx3", [P, N], F32, 28)[:])
+        for h in range(2):
+            dx[3, h] = whole[:, halves[h]]
+        for t, h in ((2, 0), (3, 0), (3, 1)):
             scatter(t, h)
         for t in range(LANES):
             store_plane(t)
@@ -247,7 +257,7 @@ def tile_attend_gml_pl_sqh_kernel(tc, xT, wd, wv, y, cw, rw, offs, out_0, out_1,
         out_words = out_1.rearrange("o p t l -> p (o t l)").bitcast(I32)
         out_s = tile("out_s", [P, T], U8)
         quads = [tile("quads%d" % c, [P, n, LANES], BF16) for c, n in enumerate(OUT_CHUNKS)]
-        out_q = [tile("out_q%d" % c, [P, n], U32) for c, n in enumerate(OUT_CHUNKS)]
+        out_q = tile("out_q", [P, T], U32)
 
         def weave(c, copy, word):
             copy(
@@ -257,8 +267,10 @@ def tile_attend_gml_pl_sqh_kernel(tc, xT, wd, wv, y, cw, rw, offs, out_0, out_1,
 
         def out_quantize(c):
             cols = slice(starts[c], starts[c] + OUT_CHUNKS[c])
-            nc.vector.quantize_mx(out=out_q[c][:].bitcast(E4M3), scales=out_s[:, cols], in_=quads[c][:].rearrange("p n l -> p (n l)"))
-            nc.sync.dma_start(out_words[:, cols], out_q[c][:].bitcast(I32))
+            nc.vector.quantize_mx(out=out_q[:, cols].bitcast(E4M3), scales=out_s[:, cols], in_=quads[c][:].rearrange("p n l -> p (n l)"))
+            if c > 0:
+                stored = slice(0 if c == 1 else cols.start, cols.stop)
+                nc.sync.dma_start(out_words[:, stored], out_q[:, stored].bitcast(I32))
 
         for k in range(VECTOR_CHUNKS, len(spans)):
             round_last(k, nc.scalar.copy)

@@ -47,14 +47,15 @@ def tile_attend_gml_pl_sqh_kernel(tc, xT, wd, wv, y, cw, rw, offs, out_0, out_1,
         y_rows = y.rearrange("(p j) i -> p j i", j=LANES)
         out_rows = out_0.rearrange("(p j) t -> p j t", j=LANES)
 
+        x_plane = [tile("x_plane%d" % j, [P, T], F32) for j in range(LANES)]
+        nc.sync.dma_start(x_plane[0][:], x_rows[:, 0, :])
         offsets = sb.tile([P, N // 16], U16, name="offsets")
         nc.sync.dma_start(offsets[:], offs)
         cw_sb = tile("cw_sb", [P, LANES], F32, tag="window2")
         nc.scalar.dma_start(cw_sb[:], cw.rearrange("(p j) o -> p (j o)", j=LANES))
         rw_sb = tile("rw_sb", [P, LANES], F32)
         nc.scalar.dma_start(rw_sb[:], rw[0:1, :].rearrange("o (p c) -> p (o c)", c=LANES))
-        x_plane = [tile("x_plane%d" % j, [P, T], F32) for j in range(LANES)]
-        for j in range(LANES):
+        for j in range(1, LANES):
             nc.sync.dma_start(x_plane[j][:], x_rows[:, j, :])
         wd_raw = tile("wd_raw", [P, LANES, V], F32)
         nc.sync.dma_start(wd_raw[:], wd_rows)
@@ -110,44 +111,42 @@ def tile_attend_gml_pl_sqh_kernel(tc, xT, wd, wv, y, cw, rw, offs, out_0, out_1,
                 out=codes[:, rows, :].rearrange("p r s -> p (r s)").bitcast(E4M3), scales=scales[:, rows, :].rearrange("p r s -> p (r s)"), in_=dealt
             )
 
-        wd_b = [tile("wd_b0", [P, PAIR], BF16)[:], placed("wd_b1", [P, 4 * PAIR], BF16, 0)[:, :PAIR]]
+        wd_b = [placed("wd_b0", [P, PAIR], BF16, 8)[:], placed("wd_b1", [P, 4 * PAIR], BF16, 0)[:, :PAIR]]
         deal(nc.vector.tensor_copy, wd_b[0], wd_raw, 0)
         deal(nc.scalar.copy, wd_b[1], wd_raw, 1)
         wd_q = tile("wd_q", [P, LANES, P], U32)
         wd_s = tile("wd_s", [P, LANES, P], U8)
         row_pairs = [slice(2 * k, 2 * k + 2) for k in range(2)]
         score = {(h, k): ps.tile([P, 2, HALF], F32, name="score%d" % (2 * h + k)) for h in range(2) for k in range(2)}
-        for k in range(2):
-            quantize_pair(wd_b[k], wd_q, wd_s, k)
-        for h in range(2):
-            for r in range(LANES):
-                nc.tensor.matmul_mx(
-                    out=score[h, r // 2][:, r % 2, :], lhsT=wd_q[:, r, :].bitcast(E4M3), lhsT_scale=wd_s[:, r, :],
-                    rhs=x_q[:, halves[h]].bitcast(E4M3), rhs_scale=x_s[:, halves[h]], start=True, stop=True,
-                )
-
-        work = placed("work", [P, LANES * N], F32, 6)
+        work = placed("work", [P, LANES * N], F32, 8)
         rows = work[:].rearrange("p (r i) -> p r i", r=LANES)
         margin = {
-            (0, 0): rows[:, 2, :], (0, 1): rows[:, 3, :],
+            (0, 0): placed("margin00", [P, N], F32, 6)[:], (0, 1): rows[:, 3, :],
             (1, 0): placed("margin10", [P, N], F32, 4)[:], (1, 1): tile("margin11", [P, N], F32)[:],
         }
         coef = [placed("coef0", [P, LANES, HALF], F32, 0)[:], rows[:, :, :HALF]]
-        wv_b = [rows[:, 3, :].bitcast(BF16), placed("wv_b1", [P, PAIR], BF16, 14)[:]]
-        g_b = [rows[:, 2, :].bitcast(BF16), placed("g_b1", [P, HALF * LANES], BF16, 14)[:]]
+        wv_b = [rows[:, 3, :].bitcast(BF16), placed("wv_b1", [P, PAIR], BF16, 16)[:]]
+        g_b = [rows[:, 2, :].bitcast(BF16), placed("g_b1", [P, HALF * LANES], BF16, 16)[:]]
         hinge = tile("hinge", [P, LANES, N], F32)
 
         def coefficients(engine, h, k):
             engine.tensor_tensor(coef[h][:, row_pairs[k], :], y_all[:, row_pairs[k], halves[h]], weight[:, row_pairs[k], halves[h]], ALU.mult)
 
+        quantize_pair(wd_b[0], wd_q, wd_s, 0)
         coefficients(nc.vector, 1, 0)
+        quantize_pair(wd_b[1], wd_q, wd_s, 1)
         for k in range(2):
             coefficients(nc.gpsimd, 0, k)
-        for h in range(2):
-            for k in range(2):
+        for k in range(2):
+            for h in range(2):
+                for r in (2 * k, 2 * k + 1):
+                    nc.tensor.matmul_mx(
+                        out=score[h, k][:, r % 2, :], lhsT=wd_q[:, r, :].bitcast(E4M3), lhsT_scale=wd_s[:, r, :],
+                        rhs=x_q[:, halves[h]].bitcast(E4M3), rhs_scale=x_s[:, halves[h]], start=True, stop=True,
+                    )
                 m = margin[h, k].rearrange("p (r i) -> p r i", r=2)
                 nc.vector.tensor_tensor(m, y_all[:, row_pairs[k], halves[h]], score[h, k][:], ALU.mult)
-                if (h, k) == (1, 0):
+                if (h, k) == (1, 1):
                     deal(nc.scalar.copy, wv_b[0], wv_raw, 0)
                 nc.scalar.activation(hinge[:, row_pairs[k], halves[h]], m, ACT.Relu, bias=1.0, scale=-1.0)
 
@@ -182,7 +181,8 @@ def tile_attend_gml_pl_sqh_kernel(tc, xT, wd, wv, y, cw, rw, offs, out_0, out_1,
 
         starts = [sum(OUT_CHUNKS[:c]) for c in range(len(OUT_CHUNKS))]
         spans = [(first, SPAN) for first in range(0, T, SPAN)]
-        pair_tiles = [tile("pairs0", [P, 2, SPAN, 2], BF16)] + [placed("pairs%d" % k, [P, 2, SPAN, 2], BF16, 12 + 4 * k) for k in range(1, len(spans))]
+        pair_tiles = [tile("pairs0", [P, 2, SPAN, 2], BF16)]
+        pair_tiles += [placed("pairs%d" % k, [P, 2, SPAN, 2], BF16, 16 + 4 * k) for k in range(1, 4)]
 
         def pairs(c):
             k, at = divmod(starts[c], SPAN)
@@ -203,7 +203,7 @@ def tile_attend_gml_pl_sqh_kernel(tc, xT, wd, wv, y, cw, rw, offs, out_0, out_1,
                 nc.vector.tensor_copy(pair_tiles[k][:, 1, :, :], src.unsqueeze(2).to_broadcast([P, n, 2]))
 
         def round_last(k, copy):
-            copy(pair_tiles[k][:, 1, :, 1], window[LAST][:, k * SPAN : (k + 1) * SPAN])
+            copy(pair_tiles[k][:, 1, :, 1], window[LAST][:, spans[k][0] : spans[k][0] + spans[k][1]])
 
         def bring(t, cols, bank_name, copy, dx=None):
             n = cols.stop - cols.start
@@ -225,8 +225,8 @@ def tile_attend_gml_pl_sqh_kernel(tc, xT, wd, wv, y, cw, rw, offs, out_0, out_1,
         quantize_pair(wv_b[0], wv_q, wv_s, 0)
         g_quantize(0)
         dx[0, 0] = bring(0, halves[0], "score0", nc.scalar.copy)
+        dx[1, 0] = bring(1, halves[0], "score1", nc.scalar.copy)
         coefficients(nc.vector, 1, 1)
-        dx[1, 0] = bring(1, halves[0], "score1", nc.vector.tensor_copy)
         g_round(1)
         g_quantize(1)
         deal(nc.vector.tensor_copy, wv_b[1], wv_raw, 1)
@@ -236,14 +236,10 @@ def tile_attend_gml_pl_sqh_kernel(tc, xT, wd, wv, y, cw, rw, offs, out_0, out_1,
         for h in range(2):
             for t in range(2):
                 scatter(t, h)
-        bank = ps.tile([P, N], F32, name="grad2")
-        back(bank[:], 2, slice(0, N))
-        dx[2, 1] = placed("dx2_vector", [P, 10 * HALF], F32, 19)[:, :HALF]
-        dx[2, 0] = tile("dx2_scalar", [P, HALF], F32)[:]
-        for h in (1, 0):
-            nc.vector.tensor_copy(dx[2, h], bank[:, halves[h]])
+        dx[2, 1] = bring(2, halves[1], "grad2", nc.vector.tensor_copy, placed("dx2_vector", [P, 10 * HALF], F32, 23)[:, :HALF])
+        dx[2, 0] = bring(2, halves[0], "score2", nc.vector.tensor_copy)
         scatter(2, 1)
-        whole = bring(3, slice(0, N), "grad3", nc.vector.tensor_copy, placed("dx3", [P, N], F32, 28)[:])
+        whole = bring(3, slice(0, N), "grad3", nc.vector.tensor_copy, placed("dx3", [P, N], F32, 32)[:])
         for h in range(2):
             dx[3, h] = whole[:, halves[h]]
         for t, h in ((2, 0), (3, 0), (3, 1)):
@@ -268,9 +264,7 @@ def tile_attend_gml_pl_sqh_kernel(tc, xT, wd, wv, y, cw, rw, offs, out_0, out_1,
         def out_quantize(c):
             cols = slice(starts[c], starts[c] + OUT_CHUNKS[c])
             nc.vector.quantize_mx(out=out_q[:, cols].bitcast(E4M3), scales=out_s[:, cols], in_=quads[c][:].rearrange("p n l -> p (n l)"))
-            if c > 0:
-                stored = slice(0 if c == 1 else cols.start, cols.stop)
-                nc.sync.dma_start(out_words[:, stored], out_q[:, stored].bitcast(I32))
+            nc.sync.dma_start(out_words[:, cols], out_q[:, cols].bitcast(I32))
 
         for k in range(VECTOR_CHUNKS, len(spans)):
             round_last(k, nc.scalar.copy)

@@ -264,7 +264,9 @@ def tile_attend_gml_pl_sqh_kernel(tc, xT, wd, wv, y, cw, rw, offs, out_0, out_1,
         def out_quantize(c):
             cols = slice(starts[c], starts[c] + OUT_CHUNKS[c])
             nc.vector.quantize_mx(out=out_q[:, cols].bitcast(E4M3), scales=out_s[:, cols], in_=quads[c][:].rearrange("p n l -> p (n l)"))
-            nc.sync.dma_start(out_words[:, cols], out_q[:, cols].bitcast(I32))
+            if cols.stop % SPAN == 0:
+                stored = slice(cols.stop - SPAN, cols.stop)
+                nc.sync.dma_start(out_words[:, stored], out_q[:, stored].bitcast(I32))
 
         for k in range(VECTOR_CHUNKS, len(spans)):
             round_last(k, nc.scalar.copy)

@@ -19,13 +19,13 @@ ACT = mybir.ActivationFunctionType
 
 P = 128
 LANES = 4
-OUT_CHUNKS = (512, 512, 512, 256, 256)
-VECTOR_CHUNKS = 2
-SPAN = 512
-GPSIMD_COLUMNS = 512
-LAST = LANES - 1
 HALF = N // 2
 PAIR = 2 * P * LANES
+OUT_CHUNKS = (512, 512, 512, 256, 256)
+VECTOR_CHUNKS = 2
+SCALAR_ENTRIES = 320
+LAST = LANES - 1
+SPAN = 512
 
 
 def tile_attend_gml_pl_sqh_kernel(tc, xT, wd, wv, y, cw, rw, offs, out_0, out_1, out_2):
@@ -33,13 +33,14 @@ def tile_attend_gml_pl_sqh_kernel(tc, xT, wd, wv, y, cw, rw, offs, out_0, out_1,
     with ExitStack() as ctx:
         sb = ctx.enter_context(tc.tile_pool(name="sb", bufs=1))
         shared = ctx.enter_context(tc.tile_pool(name="shared", bufs=1))
+        result = ctx.enter_context(tc.tile_pool(name="result", bufs=1))
         ps = ctx.enter_context(tc.psum_pool(name="ps", bufs=1))
 
         def tile(name, shape, dtype, tag=None):
             return sb.tile(shape, dtype, name=name, tag=tag or name, align_bytes=64)
 
-        def placed(name, shape, dtype, kib):
-            return shared.tile(shape, dtype, name=name, align_bytes=64, offset=1024 * kib)
+        def placed(pool, name, shape, dtype, kib):
+            return pool.tile(shape, dtype, name=name, align_bytes=64, offset=1024 * kib)
 
         x_rows = xT.rearrange("(p j) t -> p j t", j=LANES)
         wd_rows = wd.rearrange("(p j) v -> p j v", j=LANES)
@@ -51,7 +52,7 @@ def tile_attend_gml_pl_sqh_kernel(tc, xT, wd, wv, y, cw, rw, offs, out_0, out_1,
         nc.sync.dma_start(x_plane[0][:], x_rows[:, 0, :])
         offsets = sb.tile([P, N // 16], U16, name="offsets")
         nc.sync.dma_start(offsets[:], offs)
-        cw_sb = tile("cw_sb", [P, LANES], F32, tag="window2")
+        cw_sb = placed(result, "cw_sb", [P, LANES], F32, 16)
         nc.scalar.dma_start(cw_sb[:], cw.rearrange("(p j) o -> p (j o)", j=LANES))
         rw_sb = tile("rw_sb", [P, LANES], F32)
         nc.scalar.dma_start(rw_sb[:], rw[0:1, :].rearrange("o (p c) -> p (o c)", c=LANES))
@@ -65,23 +66,23 @@ def tile_attend_gml_pl_sqh_kernel(tc, xT, wd, wv, y, cw, rw, offs, out_0, out_1,
         wv_raw = tile("wv_raw", [P, LANES, D], F32)
         nc.sync.dma_start(wv_raw[:], wv_rows)
 
-        window = {t: tile("window%d" % t, [P, T], F32) for t in range(2)}
+        window = {t: placed(result, "window%d" % t, [P, T], F32, 8 * t) for t in range(2)}
         for t in range(2):
             nc.vector.memset(window[t][:], 0.0)
 
         ident = tile("ident", [P, P], F32)
         make_identity(nc, ident[:])
-        minus_one = tile("minus_one", [P, LANES], F32, tag="window3")
+        minus_one = placed(result, "minus_one", [P, LANES], F32, 24)
         nc.gpsimd.memset(minus_one[:], -1.0)
         neg_cw = tile("neg_cw", [P, LANES], F32)
         nc.gpsimd.tensor_tensor(neg_cw[:], cw_sb[:], minus_one[:], ALU.mult)
         for t in range(2, LANES):
-            window[t] = tile("window%d" % t, [P, T], F32)
+            window[t] = placed(result, "window%d" % t, [P, T], F32, 8 * t)
             nc.gpsimd.memset(window[t][:], 0.0)
         rw_all = ps.tile([P, LANES, P], F32, name="grad3")
         for c in range(LANES):
             nc.tensor.transpose(rw_all[:, c, :], rw_sb[:, c : c + 1].to_broadcast([P, P]), ident[:])
-        weight = tile("weight", [P, LANES, N], F32)
+        weight = placed(shared, "weight", [P, LANES, N], F32, 20)
         for r in range(LANES):
             nc.scalar.mul(weight[:, r, :].rearrange("m (p c) -> m p c", c=LANES), rw_all[:].rearrange("m c p -> m p c"), neg_cw[:, r : r + 1])
 
@@ -106,27 +107,22 @@ def tile_attend_gml_pl_sqh_kernel(tc, xT, wd, wv, y, cw, rw, offs, out_0, out_1,
             )
 
         def quantize_pair(dealt, codes, scales, h):
-            rows = slice(2 * h, 2 * h + 2)
-            nc.vector.quantize_mx(
-                out=codes[:, rows, :].rearrange("p r s -> p (r s)").bitcast(E4M3), scales=scales[:, rows, :].rearrange("p r s -> p (r s)"), in_=dealt
-            )
+            nc.vector.quantize_mx(out=codes[h][:].bitcast(E4M3), scales=scales[h][:], in_=dealt)
 
-        wd_b = [placed("wd_b0", [P, PAIR], BF16, 8)[:], placed("wd_b1", [P, 4 * PAIR], BF16, 0)[:, :PAIR]]
+        def group(pairs, r):
+            return pairs[r // 2][:, (r % 2) * P : (r % 2 + 1) * P]
+
+        wd_b = [placed(shared, "wd_b0", [P, PAIR], BF16, 8)[:], placed(shared, "wd_b1", [P, PAIR], BF16, 3)[:]]
         deal(nc.vector.tensor_copy, wd_b[0], wd_raw, 0)
         deal(nc.scalar.copy, wd_b[1], wd_raw, 1)
-        wd_q = tile("wd_q", [P, LANES, P], U32)
-        wd_s = tile("wd_s", [P, LANES, P], U8)
+        wd_q = [tile("wd_q%d" % h, [P, 2 * P], U32) for h in range(2)]
+        wd_s = [tile("wd_s%d" % h, [P, 2 * P], U8) for h in range(2)]
         row_pairs = [slice(2 * k, 2 * k + 2) for k in range(2)]
         score = {(h, k): ps.tile([P, 2, HALF], F32, name="score%d" % (2 * h + k)) for h in range(2) for k in range(2)}
-        work = placed("work", [P, LANES * N], F32, 8)
-        rows = work[:].rearrange("p (r i) -> p r i", r=LANES)
-        margin = {
-            (0, 0): placed("margin00", [P, N], F32, 6)[:], (0, 1): rows[:, 3, :],
-            (1, 0): placed("margin10", [P, N], F32, 4)[:], (1, 1): tile("margin11", [P, N], F32)[:],
-        }
-        coef = [placed("coef0", [P, LANES, HALF], F32, 0)[:], rows[:, :, :HALF]]
-        wv_b = [rows[:, 3, :].bitcast(BF16), placed("wv_b1", [P, PAIR], BF16, 16)[:]]
-        g_b = [rows[:, 2, :].bitcast(BF16), placed("g_b1", [P, HALF * LANES], BF16, 16)[:]]
+        margin = {(h, k): placed(shared, "margin%d%d" % (h, k), [P, N], F32, at)[:] for (h, k), at in (((0, 0), 4), ((0, 1), 12), ((1, 0), 14), ((1, 1), 16))}
+        coef = [placed(shared, "coef%d" % h, [P, LANES, HALF], F32, 8 * h)[:] for h in range(2)]
+        wv_b = [placed(shared, "wv_b0", [P, PAIR], BF16, 12)[:], placed(shared, "wv_b1", [P, PAIR], BF16, 16)[:]]
+        g_b = [placed(shared, "g_b0", [P, HALF * LANES], BF16, 18)[:], placed(shared, "g_b1", [P, HALF * LANES], BF16, 12)[:]]
         hinge = tile("hinge", [P, LANES, N], F32)
 
         def coefficients(engine, h, k):
@@ -137,16 +133,16 @@ def tile_attend_gml_pl_sqh_kernel(tc, xT, wd, wv, y, cw, rw, offs, out_0, out_1,
         quantize_pair(wd_b[1], wd_q, wd_s, 1)
         for k in range(2):
             coefficients(nc.gpsimd, 0, k)
-        for k in range(2):
-            for h in range(2):
+        for h in range(2):
+            for k in range(2):
                 for r in (2 * k, 2 * k + 1):
                     nc.tensor.matmul_mx(
-                        out=score[h, k][:, r % 2, :], lhsT=wd_q[:, r, :].bitcast(E4M3), lhsT_scale=wd_s[:, r, :],
+                        out=score[h, k][:, r % 2, :], lhsT=group(wd_q, r).bitcast(E4M3), lhsT_scale=group(wd_s, r),
                         rhs=x_q[:, halves[h]].bitcast(E4M3), rhs_scale=x_s[:, halves[h]], start=True, stop=True,
                     )
                 m = margin[h, k].rearrange("p (r i) -> p r i", r=2)
                 nc.vector.tensor_tensor(m, y_all[:, row_pairs[k], halves[h]], score[h, k][:], ALU.mult)
-                if (h, k) == (1, 1):
+                if (h, k) == (1, 0):
                     deal(nc.scalar.copy, wv_b[0], wv_raw, 0)
                 nc.scalar.activation(hinge[:, row_pairs[k], halves[h]], m, ACT.Relu, bias=1.0, scale=-1.0)
 
@@ -164,25 +160,33 @@ def tile_attend_gml_pl_sqh_kernel(tc, xT, wd, wv, y, cw, rw, offs, out_0, out_1,
         def g_quantize(h):
             nc.vector.quantize_mx(out=g_q[:, halves[h]].bitcast(E5M2), scales=g_s[:, halves[h]], in_=g_b[h])
 
-        wv_q = tile("wv_q", [P, LANES, P], U32)
-        wv_s = tile("wv_s", [P, LANES, P], U8)
+        wv_q = [tile("wv_q0", [P, 2 * P], U32), placed(shared, "wv_q1", [P, 2 * P], U32, 18)]
+        wv_s = [tile("wv_s%d" % h, [P, 2 * P], U8) for h in range(2)]
+        dx = tile("dx", [P, LANES * N], F32)
+
+        def source(t, cols):
+            return dx[:, t * N + cols.start : t * N + cols.stop]
 
         def back(bank, t, cols):
             nc.tensor.matmul_mx(
-                out=bank, lhsT=wv_q[:, t, :].bitcast(E4M3), lhsT_scale=wv_s[:, t, :],
+                out=bank, lhsT=group(wv_q, t).bitcast(E4M3), lhsT_scale=group(wv_s, t),
                 rhs=g_q[:, cols].bitcast(E5M2), rhs_scale=g_s[:, cols], start=True, stop=True,
             )
 
-        def listed(t, h):
-            return window[t][:].indirect(half_list[h])
+        def bring(t, cols, bank_name, copy):
+            bank = ps.tile([P, cols.stop - cols.start], F32, name=bank_name)
+            back(bank[:], t, cols)
+            copy(source(t, cols), bank[:])
+
+        def scalar_scatter(t, h):
+            nc.scalar.activation(window[t][:].indirect(half_list[h]), source(t, halves[h]), ACT.Copy)
 
         def store_plane(t):
             (nc.scalar if t == LAST else nc.sync).dma_start(out_rows[:, t, :], window[t][:])
 
         starts = [sum(OUT_CHUNKS[:c]) for c in range(len(OUT_CHUNKS))]
         spans = [(first, SPAN) for first in range(0, T, SPAN)]
-        pair_tiles = [tile("pairs0", [P, 2, SPAN, 2], BF16)]
-        pair_tiles += [placed("pairs%d" % k, [P, 2, SPAN, 2], BF16, 16 + 4 * k) for k in range(1, 4)]
+        pair_tiles = [tile("pairs%d" % k, [P, 2, SPAN, 2], BF16) for k in range(len(spans))]
 
         def pairs(c):
             k, at = divmod(starts[c], SPAN)
@@ -191,61 +195,44 @@ def tile_attend_gml_pl_sqh_kernel(tc, xT, wd, wv, y, cw, rw, offs, out_0, out_1,
         def round_early(t, k):
             first, n = spans[k]
             src = window[t][:, first : first + n]
-            done = min(max(GPSIMD_COLUMNS - first, 0), n) if t == 0 else 0
-            if done:
-                both = src[:, :done].unsqueeze(2).to_broadcast([P, done, 2])
-                nc.gpsimd.tensor_scalar(pair_tiles[k][:, 0, :done, :], both, 1.0, -0.0, ALU.mult, ALU.add)
-            if done == n:
-                return
             if k < VECTOR_CHUNKS or t < 2:
-                nc.vector.tensor_copy(pair_tiles[k][:, t // 2, done:, t % 2], src[:, done:])
+                nc.vector.tensor_copy(pair_tiles[k][:, t // 2, :, t % 2], src)
             else:
                 nc.vector.tensor_copy(pair_tiles[k][:, 1, :, :], src.unsqueeze(2).to_broadcast([P, n, 2]))
 
         def round_last(k, copy):
             copy(pair_tiles[k][:, 1, :, 1], window[LAST][:, spans[k][0] : spans[k][0] + spans[k][1]])
 
-        def bring(t, cols, bank_name, copy, dx=None):
-            n = cols.stop - cols.start
-            bank = ps.tile([P, n], F32, name=bank_name)
-            back(bank[:], t, cols)
-            if dx is None:
-                dx = tile("dx%d_%d" % (t, cols.start), [P, n], F32)[:]
-            copy(dx, bank[:])
-            return dx
+        zero = tile("zero", [P, N - SCALAR_ENTRIES], F32)
+        nc.gpsimd.memset(zero[:], 0.0)
 
-        def scatter(t, h):
-            if (t, h) == (2, 1):
-                nc.vector.tensor_copy(listed(t, h), dx[t, h])
-            else:
-                nc.scalar.activation(listed(t, h), dx[t, h], ACT.Copy)
-
-        dx = {}
+        deal(nc.scalar.copy, wv_b[1], wv_raw, 1)
         g_round(0)
         quantize_pair(wv_b[0], wv_q, wv_s, 0)
         g_quantize(0)
-        dx[0, 0] = bring(0, halves[0], "score0", nc.scalar.copy)
-        dx[1, 0] = bring(1, halves[0], "score1", nc.scalar.copy)
+        for t in range(2):
+            bring(t, halves[0], "score%d" % t, nc.scalar.copy)
+        scalar_scatter(0, 0)
+        scalar_scatter(1, 0)
         coefficients(nc.vector, 1, 1)
-        g_round(1)
-        g_quantize(1)
-        deal(nc.vector.tensor_copy, wv_b[1], wv_raw, 1)
-        dx[0, 1] = bring(0, halves[1], "grad0", nc.vector.tensor_copy)
         quantize_pair(wv_b[1], wv_q, wv_s, 1)
-        dx[1, 1] = bring(1, halves[1], "grad1", nc.vector.tensor_copy)
-        for h in range(2):
-            for t in range(2):
-                scatter(t, h)
-        dx[2, 1] = bring(2, halves[1], "grad2", nc.vector.tensor_copy, placed("dx2_vector", [P, 10 * HALF], F32, 23)[:, :HALF])
-        dx[2, 0] = bring(2, halves[0], "score2", nc.vector.tensor_copy)
-        scatter(2, 1)
-        whole = bring(3, slice(0, N), "grad3", nc.vector.tensor_copy, placed("dx3", [P, N], F32, 32)[:])
-        for h in range(2):
-            dx[3, h] = whole[:, halves[h]]
-        for t, h in ((2, 0), (3, 0), (3, 1)):
-            scatter(t, h)
+        g_round(1)
+        bring(2, halves[0], "score2", nc.vector.tensor_copy)
+        g_quantize(1)
+        bring(3, halves[0], "score3", nc.vector.tensor_copy)
+        for t in range(2):
+            bring(t, halves[1], "grad%d" % t, nc.vector.tensor_copy)
+        nc.vector.tensor_copy(window[0][:].indirect(half_list[1]), source(0, halves[1]))
+        store_plane(0)
+        for t in (3, 2):
+            bring(t, halves[1], "grad%d" % t, nc.vector.tensor_copy)
+        nc.vector.tensor_tensor(window[LAST][:].indirect(offsets[:, SCALAR_ENTRIES // 16 :]), source(LAST, slice(SCALAR_ENTRIES, N)), zero[:], ALU.add)
+        for t, h in ((2, 0), (1, 1), (2, 1)):
+            scalar_scatter(t, h)
+        nc.scalar.activation(window[LAST][:].indirect(offsets[:, : SCALAR_ENTRIES // 16]), source(LAST, slice(0, SCALAR_ENTRIES)), ACT.Copy)
         for t in range(LANES):
-            store_plane(t)
+            if t:
+                store_plane(t)
             if t != LAST:
                 for k in range(len(spans)):
                     round_early(t, k)

@@ -82,9 +82,12 @@ def tile_attend_gml_pl_sqh_kernel(tc, xT, wd, wv, y, cw, rw, offs, out_0, out_1,
         rw_all = ps.tile([P, LANES, P], F32, name="grad3")
         for c in range(LANES):
             nc.tensor.transpose(rw_all[:, c, :], rw_sb[:, c : c + 1].to_broadcast([P, P]), ident[:])
-        weight = placed(shared, "weight", [P, LANES, N], F32, 20)
+        rw_list = rw_all[:].rearrange("m c p -> m p c")
+        weight = tile("weight", [P, LANES, HALF], F32)
         for r in range(LANES):
-            nc.scalar.mul(weight[:, r, :].rearrange("m (p c) -> m p c", c=LANES), rw_all[:].rearrange("m c p -> m p c"), neg_cw[:, r : r + 1])
+            nc.scalar.mul(weight[:, r, :].rearrange("m (p c) -> m p c", c=LANES), rw_list[:, : HALF // LANES, :], neg_cw[:, r : r + 1])
+        late_weight = tile("late_weight", [P, HALF], F32)
+        nc.scalar.mul(late_weight[:].rearrange("m (p c) -> m p c", c=LANES), rw_list[:, HALF // LANES :, :], neg_cw[:, LAST : LAST + 1])
 
         x_b = tile("x_b", [P, N, LANES], BF16)
         halves = [slice(h * HALF, (h + 1) * HALF) for h in range(2)]
@@ -125,14 +128,22 @@ def tile_attend_gml_pl_sqh_kernel(tc, xT, wd, wv, y, cw, rw, offs, out_0, out_1,
         g_b = [placed(shared, "g_b0", [P, HALF * LANES], BF16, 18)[:], placed(shared, "g_b1", [P, HALF * LANES], BF16, 12)[:]]
         hinge = tile("hinge", [P, LANES, N], F32)
 
-        def coefficients(engine, h, k):
-            engine.tensor_tensor(coef[h][:, row_pairs[k], :], y_all[:, row_pairs[k], halves[h]], weight[:, row_pairs[k], halves[h]], ALU.mult)
+        def early_coefficients(k):
+            nc.gpsimd.tensor_tensor(coef[0][:, row_pairs[k], :], y_all[:, row_pairs[k], halves[0]], weight[:, row_pairs[k], :], ALU.mult)
+
+        def late_coefficients(rows):
+            for r in rows:
+                nc.vector.scalar_tensor_tensor(
+                    coef[1][:, r, :].rearrange("m (p c) -> m p c", c=LANES), y_all[:, r, halves[1]].rearrange("m (p c) -> m p c", c=LANES),
+                    neg_cw[:, r : r + 1], rw_list[:, HALF // LANES :, :], ALU.mult, ALU.mult,
+                )
 
         quantize_pair(wd_b[0], wd_q, wd_s, 0)
-        coefficients(nc.vector, 1, 0)
         quantize_pair(wd_b[1], wd_q, wd_s, 1)
+        late_coefficients((0, 1))
         for k in range(2):
-            coefficients(nc.gpsimd, 0, k)
+            early_coefficients(k)
+        nc.gpsimd.tensor_tensor(coef[1][:, LAST, :], y_all[:, LAST, halves[1]], late_weight[:], ALU.mult)
         for h in range(2):
             for k in range(2):
                 for r in (2 * k, 2 * k + 1):
@@ -214,7 +225,7 @@ def tile_attend_gml_pl_sqh_kernel(tc, xT, wd, wv, y, cw, rw, offs, out_0, out_1,
             bring(t, halves[0], "score%d" % t, nc.scalar.copy)
         scalar_scatter(0, 0)
         scalar_scatter(1, 0)
-        coefficients(nc.vector, 1, 1)
+        late_coefficients((2,))
         quantize_pair(wv_b[1], wv_q, wv_s, 1)
         g_round(1)
         bring(2, halves[0], "score2", nc.vector.tensor_copy)

@@ -23,7 +23,6 @@ HALF = N // 2
 PAIR = 2 * P * LANES
 OUT_CHUNKS = (512, 512, 512, 256, 256)
 VECTOR_CHUNKS = 2
-SCALAR_ENTRIES = 320
 LAST = LANES - 1
 SPAN = 512
 
@@ -126,7 +125,7 @@ def tile_attend_gml_pl_sqh_kernel(tc, xT, wd, wv, y, cw, rw, offs, out_0, out_1,
         coef = [placed(shared, "coef%d" % h, [P, LANES, HALF], F32, 8 * h)[:] for h in range(2)]
         wv_b = [placed(shared, "wv_b0", [P, PAIR], BF16, 12)[:], placed(shared, "wv_b1", [P, PAIR], BF16, 16)[:]]
         g_b = [placed(shared, "g_b0", [P, HALF * LANES], BF16, 18)[:], placed(shared, "g_b1", [P, HALF * LANES], BF16, 12)[:]]
-        hinge = tile("hinge", [P, LANES, N], F32)
+        hinge = [tile("hinge%d" % h, [P, LANES, HALF], F32) for h in range(2)]
 
         def early_coefficients(k):
             nc.gpsimd.tensor_tensor(coef[0][:, row_pairs[k], :], y_all[:, row_pairs[k], halves[0]], weight[:, row_pairs[k], :], ALU.mult)
@@ -155,7 +154,7 @@ def tile_attend_gml_pl_sqh_kernel(tc, xT, wd, wv, y, cw, rw, offs, out_0, out_1,
                 nc.vector.tensor_tensor(m, y_all[:, row_pairs[k], halves[h]], score[h, k][:], ALU.mult)
                 if (h, k) == (1, 0):
                     deal(nc.scalar.copy, wv_b[0], wv_raw, 0)
-                nc.scalar.activation(hinge[:, row_pairs[k], halves[h]], m, ACT.Relu, bias=1.0, scale=-1.0)
+                nc.scalar.activation(hinge[h][:, row_pairs[k], :], m, ACT.Relu, bias=1.0, scale=-1.0)
 
         g_q = tile("g_q", [P, N], U32)
         g_s = tile("g_s", [P, N], U8)
@@ -163,7 +162,7 @@ def tile_attend_gml_pl_sqh_kernel(tc, xT, wd, wv, y, cw, rw, offs, out_0, out_1,
         def g_round(h):
             nc.vector.tensor_tensor(
                 g_b[h].rearrange("p (c i r) -> p c r i", i=4, r=LANES),
-                hinge[:, :, halves[h]].rearrange("p r (c i) -> p c r i", i=4),
+                hinge[h][:].rearrange("p r (c i) -> p c r i", i=4),
                 coef[h].rearrange("p r (c i) -> p c r i", i=4),
                 ALU.mult,
             )
@@ -206,16 +205,17 @@ def tile_attend_gml_pl_sqh_kernel(tc, xT, wd, wv, y, cw, rw, offs, out_0, out_1,
         def round_early(t, k):
             first, n = spans[k]
             src = window[t][:, first : first + n]
-            if k < VECTOR_CHUNKS or t < 2:
+            if (t, k) == (0, 0):
+                nc.gpsimd.tensor_scalar(pair_tiles[k][:, 0, :, :], src.unsqueeze(2).to_broadcast([P, n, 2]), 1.0, -0.0, ALU.mult, ALU.add)
+            elif k < VECTOR_CHUNKS or t < 2:
                 nc.vector.tensor_copy(pair_tiles[k][:, t // 2, :, t % 2], src)
+            elif k == len(spans) - 1:
+                nc.scalar.copy(pair_tiles[k][:, 1, :, 0], src)
             else:
                 nc.vector.tensor_copy(pair_tiles[k][:, 1, :, :], src.unsqueeze(2).to_broadcast([P, n, 2]))
 
         def round_last(k, copy):
             copy(pair_tiles[k][:, 1, :, 1], window[LAST][:, spans[k][0] : spans[k][0] + spans[k][1]])
-
-        zero = tile("zero", [P, N - SCALAR_ENTRIES], F32)
-        nc.gpsimd.memset(zero[:], 0.0)
 
         deal(nc.scalar.copy, wv_b[1], wv_raw, 1)
         g_round(0)
@@ -237,10 +237,9 @@ def tile_attend_gml_pl_sqh_kernel(tc, xT, wd, wv, y, cw, rw, offs, out_0, out_1,
         store_plane(0)
         for t in (3, 2):
             bring(t, halves[1], "grad%d" % t, nc.vector.tensor_copy)
-        nc.vector.tensor_tensor(window[LAST][:].indirect(offsets[:, SCALAR_ENTRIES // 16 :]), source(LAST, slice(SCALAR_ENTRIES, N)), zero[:], ALU.add)
-        for t, h in ((2, 0), (1, 1), (2, 1)):
+        nc.vector.tensor_copy(window[LAST][:].indirect(half_list[1]), source(LAST, halves[1]))
+        for t, h in ((2, 0), (1, 1), (2, 1), (3, 0)):
             scalar_scatter(t, h)
-        nc.scalar.activation(window[LAST][:].indirect(offsets[:, : SCALAR_ENTRIES // 16]), source(LAST, slice(0, SCALAR_ENTRIES)), ACT.Copy)
         for t in range(LANES):
             if t:
                 store_plane(t)

@@ -235,11 +235,12 @@ def tile_attend_gml_pl_sqh_kernel(tc, xT, wd, wv, y, cw, rw, offs, out_0, out_1,
             bring(t, halves[1], "grad%d" % t, nc.vector.tensor_copy)
         nc.vector.tensor_copy(window[0][:].indirect(half_list[1]), source(0, halves[1]))
         store_plane(0)
-        for t in (3, 2):
+        nc.vector.tensor_copy(window[1][:].indirect(half_list[1]), source(1, halves[1]))
+        for t in range(2, LANES):
             bring(t, halves[1], "grad%d" % t, nc.vector.tensor_copy)
-        nc.vector.tensor_copy(window[LAST][:].indirect(half_list[1]), source(LAST, halves[1]))
-        for t, h in ((2, 0), (1, 1), (2, 1), (3, 0)):
-            scalar_scatter(t, h)
+        for h in range(2):
+            for t in range(2, LANES):
+                scalar_scatter(t, h)
         for t in range(LANES):
             if t:
                 store_plane(t)

@@ -24,6 +24,8 @@ PAIR = 2 * P * LANES
 OUT_CHUNKS = (512, 512, 512, 256, 256)
 VECTOR_CHUNKS = 2
 LAST = LANES - 1
+GPSIMD_COLUMNS = 768
+VECTOR_EXTRA = 128
 SPAN = 512
 
 
@@ -205,10 +207,13 @@ def tile_attend_gml_pl_sqh_kernel(tc, xT, wd, wv, y, cw, rw, offs, out_0, out_1,
         def round_early(t, k):
             first, n = spans[k]
             src = window[t][:, first : first + n]
-            if (t, k) == (0, 0):
-                nc.gpsimd.tensor_scalar(pair_tiles[k][:, 0, :, :], src.unsqueeze(2).to_broadcast([P, n, 2]), 1.0, -0.0, ALU.mult, ALU.add)
-            elif k < VECTOR_CHUNKS or t < 2:
-                nc.vector.tensor_copy(pair_tiles[k][:, t // 2, :, t % 2], src)
+            done = min(max(GPSIMD_COLUMNS - first, 0), n) if t == 0 else 0
+            if done:
+                nc.gpsimd.tensor_scalar(pair_tiles[k][:, 0, :done, :], src[:, :done].unsqueeze(2).to_broadcast([P, done, 2]), 1.0, -0.0, ALU.mult, ALU.add)
+            if done == n:
+                return
+            if k < VECTOR_CHUNKS or t < 2:
+                nc.vector.tensor_copy(pair_tiles[k][:, t // 2, done:, t % 2], src[:, done:])
             elif k == len(spans) - 1:
                 nc.scalar.copy(pair_tiles[k][:, 1, :, 0], src)
             else:
@@ -253,10 +258,10 @@ def tile_attend_gml_pl_sqh_kernel(tc, xT, wd, wv, y, cw, rw, offs, out_0, out_1,
         quads = [tile("quads%d" % c, [P, n, LANES], BF16) for c, n in enumerate(OUT_CHUNKS)]
         out_q = tile("out_q", [P, T], U32)
 
-        def weave(c, copy, word):
+        def weave(c, copy, word, cols=slice(None)):
             copy(
-                quads[c][:].rearrange("p n l -> p (n l)").bitcast(word).rearrange("p (c i u) -> p c u i", i=2, u=2),
-                pairs(c).rearrange("p u n e -> p u (n e)").bitcast(word).rearrange("p u (c i) -> p c u i", i=2),
+                quads[c][:, cols, :].rearrange("p n l -> p (n l)").bitcast(word).rearrange("p (c i u) -> p c u i", i=2, u=2),
+                pairs(c)[:, :, cols, :].rearrange("p u n e -> p u (n e)").bitcast(word).rearrange("p u (c i) -> p c u i", i=2),
             )
 
         def out_quantize(c):
@@ -268,12 +273,14 @@ def tile_attend_gml_pl_sqh_kernel(tc, xT, wd, wv, y, cw, rw, offs, out_0, out_1,
 
         for k in range(VECTOR_CHUNKS, len(spans)):
             round_last(k, nc.scalar.copy)
-        for c in range(VECTOR_CHUNKS, len(OUT_CHUNKS)):
+        weave(VECTOR_CHUNKS, nc.scalar.copy, U32, slice(VECTOR_EXTRA, SPAN))
+        for c in range(VECTOR_CHUNKS + 1, len(OUT_CHUNKS)):
             weave(c, nc.scalar.copy, U32)
         for c in range(VECTOR_CHUNKS):
             round_last(c, nc.vector.tensor_copy)
         for c in range(VECTOR_CHUNKS):
             weave(c, nc.vector.tensor_copy, I32)
+        weave(VECTOR_CHUNKS, nc.vector.tensor_copy, I32, slice(0, VECTOR_EXTRA))
         for c in range(len(OUT_CHUNKS)):
             out_quantize(c)
         for q in range(4):

from contextlib import ExitStack

import concourse.mybir as mybir
from concourse.masks import make_identity

N, T, D, V = 512, 2048, 512, 512
FLOPS = 2 * 2 * D * V * N

F32 = mybir.dt.float32
BF16 = mybir.dt.bfloat16
I32 = mybir.dt.int32
U32 = mybir.dt.uint32
U16 = mybir.dt.uint16
U8 = mybir.dt.uint8
E4M3 = mybir.dt.float8_e4m3fn_x4
E5M2 = mybir.dt.float8_e5m2_x4
ALU = mybir.AluOpType
ACT = mybir.ActivationFunctionType

P = 128
LANES = 4
HALF = N // 2
PAIR = 2 * P * LANES
OUT_CHUNKS = (512, 512, 512, 256, 256)
VECTOR_CHUNKS = 2
LAST = LANES - 1
GPSIMD_COLUMNS = 768
VECTOR_EXTRA = 128
SPAN = 512


def tile_attend_gml_pl_sqh_kernel(tc, xT, wd, wv, y, cw, rw, offs, out_0, out_1, out_2):
    nc = tc.nc
    with ExitStack() as ctx:
        sb = ctx.enter_context(tc.tile_pool(name="sb", bufs=1))
        shared = ctx.enter_context(tc.tile_pool(name="shared", bufs=1))
        result = ctx.enter_context(tc.tile_pool(name="result", bufs=1))
        ps = ctx.enter_context(tc.psum_pool(name="ps", bufs=1))

        def tile(name, shape, dtype, tag=None):
            return sb.tile(shape, dtype, name=name, tag=tag or name, align_bytes=64)

        def placed(pool, name, shape, dtype, kib):
            return pool.tile(shape, dtype, name=name, align_bytes=64, offset=1024 * kib)

        x_rows = xT.rearrange("(p j) t -> p j t", j=LANES)
        wd_rows = wd.rearrange("(p j) v -> p j v", j=LANES)
        wv_rows = wv.rearrange("(p j) d -> p j d", j=LANES)
        y_rows = y.rearrange("(p j) i -> p j i", j=LANES)
        out_rows = out_0.rearrange("(p j) t -> p j t", j=LANES)

        x_plane = [tile("x_plane%d" % j, [P, T], F32) for j in range(LANES)]
        nc.sync.dma_start(x_plane[0][:], x_rows[:, 0, :])
        offsets = sb.tile([P, N // 16], U16, name="offsets")
        nc.sync.dma_start(offsets[:], offs)
        cw_sb = placed(result, "cw_sb", [P, LANES], F32, 16)
        nc.scalar.dma_start(cw_sb[:], cw.rearrange("(p j) o -> p (j o)", j=LANES))
        rw_sb = tile("rw_sb", [P, LANES], F32)
        nc.scalar.dma_start(rw_sb[:], rw[0:1, :].rearrange("o (p c) -> p (o c)", c=LANES))
        for j in range(1, LANES):
            nc.sync.dma_start(x_plane[j][:], x_rows[:, j, :])
        wd_raw = tile("wd_raw", [P, LANES, V], F32)
        nc.sync.dma_start(wd_raw[:], wd_rows)
        y_all = tile("y_all", [P, LANES, N], F32)
        for h in range(2):
            nc.sync.dma_start(y_all[:, 2 * h : 2 * h + 2, :], y_rows[:, 2 * h : 2 * h + 2, :])
        wv_raw = tile("wv_raw", [P, LANES, D], F32)
        nc.sync.dma_start(wv_raw[:], wv_rows)

        window = {t: placed(result, "window%d" % t, [P, T], F32, 8 * t) for t in range(2)}
        for t in range(2):
            nc.vector.memset(window[t][:], 0.0)

        ident = tile("ident", [P, P], F32)
        make_identity(nc, ident[:])
        minus_one = placed(result, "minus_one", [P, LANES], F32, 24)
        nc.gpsimd.memset(minus_one[:], -1.0)
        neg_cw = tile("neg_cw", [P, LANES], F32)
        nc.gpsimd.tensor_tensor(neg_cw[:], cw_sb[:], minus_one[:], ALU.mult)
        for t in range(2, LANES):
            window[t] = placed(result, "window%d" % t, [P, T], F32, 8 * t)
            nc.gpsimd.memset(window[t][:], 0.0)
        rw_all = ps.tile([P, LANES, P], F32, name="grad3")
        for c in range(LANES):
            nc.tensor.transpose(rw_all[:, c, :], rw_sb[:, c : c + 1].to_broadcast([P, P]), ident[:])
        rw_list = rw_all[:].rearrange("m c p -> m p c")
        weight = tile("weight", [P, LANES, HALF], F32)
        for r in range(LANES):
            nc.scalar.mul(weight[:, r, :].rearrange("m (p c) -> m p c", c=LANES), rw_list[:, : HALF // LANES, :], neg_cw[:, r : r + 1])
        late_weight = tile("late_weight", [P, HALF], F32)
        nc.scalar.mul(late_weight[:].rearrange("m (p c) -> m p c", c=LANES), rw_list[:, HALF // LANES :, :], neg_cw[:, LAST : LAST + 1])

        x_b = tile("x_b", [P, N, LANES], BF16)
        halves = [slice(h * HALF, (h + 1) * HALF) for h in range(2)]
        half_list = [offsets[:, h * HALF // 16 : (h + 1) * HALF // 16] for h in range(2)]
        for j in range(LANES - 1):
            nc.vector.tensor_copy(x_b[:, :, j], x_plane[j][:].indirect(offsets[:]))
        for h in range(2):
            nc.vector.tensor_copy(x_b[:, halves[h], LANES - 1], x_plane[LANES - 1][:].indirect(half_list[h]))
        x_q = tile("x_q", [P, N], U32)
        x_s = tile("x_s", [P, N], U8)
        for h in range(2):
            nc.vector.quantize_mx(
                out=x_q[:, halves[h]].bitcast(E4M3), scales=x_s[:, halves[h]], in_=x_b[:, halves[h], :].rearrange("p n j -> p (n j)")
            )

        def deal(copy, dealt, raw, h):
            copy(
                dealt.rearrange("p (r s j) -> p s j r", r=2, j=LANES),
                raw[:].rearrange("p j (s r) -> p s j r", r=LANES)[:, :, :, 2 * h : 2 * h + 2],
            )

        def quantize_pair(dealt, codes, scales, h):
            nc.vector.quantize_mx(out=codes[h][:].bitcast(E4M3), scales=scales[h][:], in_=dealt)

        def group(pairs, r):
            return pairs[r // 2][:, (r % 2) * P : (r % 2 + 1) * P]

        wd_b = [placed(shared, "wd_b0", [P, PAIR], BF16, 8)[:], placed(shared, "wd_b1", [P, PAIR], BF16, 3)[:]]
        deal(nc.vector.tensor_copy, wd_b[0], wd_raw, 0)
        deal(nc.scalar.copy, wd_b[1], wd_raw, 1)
        wd_q = [tile("wd_q%d" % h, [P, 2 * P], U32) for h in range(2)]
        wd_s = [tile("wd_s%d" % h, [P, 2 * P], U8) for h in range(2)]
        row_pairs = [slice(2 * k, 2 * k + 2) for k in range(2)]
        score = {(h, k): ps.tile([P, 2, HALF], F32, name="score%d" % (2 * h + k)) for h in range(2) for k in range(2)}
        margin = {(h, k): placed(shared, "margin%d%d" % (h, k), [P, N], F32, at)[:] for (h, k), at in (((0, 0), 4), ((0, 1), 12), ((1, 0), 14), ((1, 1), 16))}
        coef = [placed(shared, "coef%d" % h, [P, LANES, HALF], F32, 8 * h)[:] for h in range(2)]
        wv_b = [placed(shared, "wv_b0", [P, PAIR], BF16, 12)[:], placed(shared, "wv_b1", [P, PAIR], BF16, 16)[:]]
        g_b = [placed(shared, "g_b0", [P, HALF * LANES], BF16, 18)[:], placed(shared, "g_b1", [P, HALF * LANES], BF16, 12)[:]]
        hinge = [tile("hinge%d" % h, [P, LANES, HALF], F32) for h in range(2)]

        def early_coefficients(k):
            nc.gpsimd.tensor_tensor(coef[0][:, row_pairs[k], :], y_all[:, row_pairs[k], halves[0]], weight[:, row_pairs[k], :], ALU.mult)

        def late_coefficients(rows):
            for r in rows:
                nc.vector.scalar_tensor_tensor(
                    coef[1][:, r, :].rearrange("m (p c) -> m p c", c=LANES), y_all[:, r, halves[1]].rearrange("m (p c) -> m p c", c=LANES),
                    neg_cw[:, r : r + 1], rw_list[:, HALF // LANES :, :], ALU.mult, ALU.mult,
                )

        quantize_pair(wd_b[0], wd_q, wd_s, 0)
        quantize_pair(wd_b[1], wd_q, wd_s, 1)
        late_coefficients((0, 1))
        for k in range(2):
            early_coefficients(k)
        nc.gpsimd.tensor_tensor(coef[1][:, LAST, :], y_all[:, LAST, halves[1]], late_weight[:], ALU.mult)
        for h in range(2):
            for k in range(2):
                for r in (2 * k, 2 * k + 1):
                    nc.tensor.matmul_mx(
                        out=score[h, k][:, r % 2, :], lhsT=group(wd_q, r).bitcast(E4M3), lhsT_scale=group(wd_s, r),
                        rhs=x_q[:, halves[h]].bitcast(E4M3), rhs_scale=x_s[:, halves[h]], start=True, stop=True,
                    )
                m = margin[h, k].rearrange("p (r i) -> p r i", r=2)
                nc.vector.tensor_tensor(m, y_all[:, row_pairs[k], halves[h]], score[h, k][:], ALU.mult)
                if (h, k) == (1, 0):
                    deal(nc.scalar.copy, wv_b[0], wv_raw, 0)
                nc.scalar.activation(hinge[h][:, row_pairs[k], :], m, ACT.Relu, bias=1.0, scale=-1.0)

        g_q = tile("g_q", [P, N], U32)
        g_s = tile("g_s", [P, N], U8)

        def g_round(h):
            nc.vector.tensor_tensor(
                g_b[h].rearrange("p (c i r) -> p c r i", i=4, r=LANES),
                hinge[h][:].rearrange("p r (c i) -> p c r i", i=4),
                coef[h].rearrange("p r (c i) -> p c r i", i=4),
                ALU.mult,
            )

        def g_quantize(h):
            nc.vector.quantize_mx(out=g_q[:, halves[h]].bitcast(E5M2), scales=g_s[:, halves[h]], in_=g_b[h])

        wv_q = [tile("wv_q0", [P, 2 * P], U32), placed(shared, "wv_q1", [P, 2 * P], U32, 18)]
        wv_s = [tile("wv_s%d" % h, [P, 2 * P], U8) for h in range(2)]
        dx = tile("dx", [P, LANES * N], F32)

        def source(t, cols):
            return dx[:, t * N + cols.start : t * N + cols.stop]

        def back(bank, t, cols):
            nc.tensor.matmul_mx(
                out=bank, lhsT=group(wv_q, t).bitcast(E4M3), lhsT_scale=group(wv_s, t),
                rhs=g_q[:, cols].bitcast(E5M2), rhs_scale=g_s[:, cols], start=True, stop=True,
            )

        def bring(t, cols, bank_name, copy):
            bank = ps.tile([P, cols.stop - cols.start], F32, name=bank_name)
            back(bank[:], t, cols)
            copy(source(t, cols), bank[:])

        def scalar_scatter(t, h):
            nc.scalar.activation(window[t][:].indirect(half_list[h]), source(t, halves[h]), ACT.Copy)

        def store_plane(t):
            (nc.scalar if t == LAST else nc.sync).dma_start(out_rows[:, t, :], window[t][:])

        starts = [sum(OUT_CHUNKS[:c]) for c in range(len(OUT_CHUNKS))]
        spans = [(first, SPAN) for first in range(0, T, SPAN)]
        pair_tiles = [tile("pairs%d" % k, [P, 2, SPAN, 2], BF16) for k in range(len(spans))]

        def pairs(c):
            k, at = divmod(starts[c], SPAN)
            return pair_tiles[k][:, :, at : at + OUT_CHUNKS[c], :]

        def round_early(t, k):
            first, n = spans[k]
            src = window[t][:, first : first + n]
            done = min(max(GPSIMD_COLUMNS - first, 0), n) if t == 0 else 0
            if done:
                nc.gpsimd.tensor_scalar(pair_tiles[k][:, 0, :done, :], src[:, :done].unsqueeze(2).to_broadcast([P, done, 2]), 1.0, -0.0, ALU.mult, ALU.add)
            if done == n:
                return
            if k < VECTOR_CHUNKS or t < 2:
                nc.vector.tensor_copy(pair_tiles[k][:, t // 2, done:, t % 2], src[:, done:])
            elif k == len(spans) - 1:
                nc.scalar.copy(pair_tiles[k][:, 1, :, 0], src)
            else:
                nc.vector.tensor_copy(pair_tiles[k][:, 1, :, :], src.unsqueeze(2).to_broadcast([P, n, 2]))

        def round_last(k, copy):
            copy(pair_tiles[k][:, 1, :, 1], window[LAST][:, spans[k][0] : spans[k][0] + spans[k][1]])

        deal(nc.scalar.copy, wv_b[1], wv_raw, 1)
        g_round(0)
        quantize_pair(wv_b[0], wv_q, wv_s, 0)
        g_quantize(0)
        for t in range(2):
            bring(t, halves[0], "score%d" % t, nc.scalar.copy)
        scalar_scatter(0, 0)
        scalar_scatter(1, 0)
        late_coefficients((2,))
        quantize_pair(wv_b[1], wv_q, wv_s, 1)
        g_round(1)
        bring(2, halves[0], "score2", nc.vector.tensor_copy)
        g_quantize(1)
        bring(3, halves[0], "score3", nc.vector.tensor_copy)
        for t in range(2):
            bring(t, halves[1], "grad%d" % t, nc.vector.tensor_copy)
        nc.vector.tensor_copy(window[0][:].indirect(half_list[1]), source(0, halves[1]))
        store_plane(0)
        nc.vector.tensor_copy(window[1][:].indirect(half_list[1]), source(1, halves[1]))
        for t in range(2, LANES):
            bring(t, halves[1], "grad%d" % t, nc.vector.tensor_copy)
        for h in range(2):
            for t in range(2, LANES):
                scalar_scatter(t, h)
        for t in range(LANES):
            if t:
                store_plane(t)
            if t != LAST:
                for k in range(len(spans)):
                    round_early(t, k)

        out_words = out_1.rearrange("o p t l -> p (o t l)").bitcast(I32)
        out_s = tile("out_s", [P, T], U8)
        quads = [tile("quads%d" % c, [P, n, LANES], BF16) for c, n in enumerate(OUT_CHUNKS)]
        out_q = tile("out_q", [P, T], U32)

        def weave(c, copy, word, cols=slice(None)):
            copy(
                quads[c][:, cols, :].rearrange("p n l -> p (n l)").bitcast(word).rearrange("p (c i u) -> p c u i", i=2, u=2),
                pairs(c)[:, :, cols, :].rearrange("p u n e -> p u (n e)").bitcast(word).rearrange("p u (c i) -> p c u i", i=2),
            )

        def out_quantize(c):
            cols = slice(starts[c], starts[c] + OUT_CHUNKS[c])
            nc.vector.quantize_mx(out=out_q[:, cols].bitcast(E4M3), scales=out_s[:, cols], in_=quads[c][:].rearrange("p n l -> p (n l)"))
            if cols.stop % SPAN == 0:
                stored = slice(cols.stop - SPAN, cols.stop)
                nc.sync.dma_start(out_words[:, stored], out_q[:, stored].bitcast(I32))

        for k in range(VECTOR_CHUNKS, len(spans)):
            round_last(k, nc.scalar.copy)
        weave(VECTOR_CHUNKS, nc.scalar.copy, U32, slice(VECTOR_EXTRA, SPAN))
        for c in range(VECTOR_CHUNKS + 1, len(OUT_CHUNKS)):
            weave(c, nc.scalar.copy, U32)
        for c in range(VECTOR_CHUNKS):
            round_last(c, nc.vector.tensor_copy)
        for c in range(VECTOR_CHUNKS):
            weave(c, nc.vector.tensor_copy, I32)
        weave(VECTOR_CHUNKS, nc.vector.tensor_copy, I32, slice(0, VECTOR_EXTRA))
        for c in range(len(OUT_CHUNKS)):
            out_quantize(c)
        for q in range(4):
            queue = nc.scalar if q % 2 else nc.sync
            queue.dma_start(out_2[0, 4 * q : 4 * q + 4, :].bitcast(I32), out_s[32 * q : 32 * q + 4, :].bitcast(I32))
